import numpy as np
import ml_dtypes


def mxq(x, axis, fmt="e4m3"):
    dtype, down = {"e4m3": (ml_dtypes.float8_e4m3fn, 7), "e5m2": (ml_dtypes.float8_e5m2, 14)}[fmt]
    v = np.moveaxis(np.asarray(x, np.float32).astype(ml_dtypes.bfloat16).astype(np.float64), axis, -1)
    blocks = v.reshape(v.shape[:-1] + (-1, 32))
    amax = np.abs(blocks).max(-1, keepdims=True)
    byte = np.maximum(np.where(amax > 0, np.frexp(amax)[1] - 1 + 127, 0) - down, 1)
    scale = np.exp2(byte - 127.0)
    codes = (blocks / scale).astype(np.float32).astype(dtype).astype(np.float64)
    return np.moveaxis((codes * scale).reshape(v.shape), -1, axis)


WIDE = False


def mx_kscale(k):
    if not WIDE:
        return np.ones(k)
    levels = np.array([10, -10, 5, -5, 0])
    if k % 512:
        return np.exp2(np.random.permutation(np.resize(levels, k // 32))).repeat(32)
    a = np.empty((k // 512, 16))
    for p in range(k // 512):
        a[p, :8] = np.random.permutation(np.resize(levels, 8))
        for g in range(8):
            far = levels[np.abs(levels - a[p, g]) >= 10]
            a[p, g + 8] = far[np.random.randint(len(far))]
    return np.exp2(a.ravel()).repeat(32)


def f64(x):
    return np.asarray(x).astype(np.float64)


def striped(idx):
    return np.tile(idx.reshape(-1, 16).T, (8, 1)).astype(np.uint16)


def unstriped(offs):
    return offs[:16].T.reshape(-1).astype(np.int64)


E2M1 = np.array([0.0, 0.5, 1.0, 1.5, 2.0, 3.0, 4.0, 6.0, -0.0, -0.5, -1.0, -1.5, -2.0, -3.0, -4.0, -6.0])


def pack_fp4(w):
    k, n = w.shape
    w = f64(np.asarray(w, np.float32).astype(ml_dtypes.bfloat16)).reshape(k // 32, 32, n)
    amax = np.abs(w).max(1)
    mant, ex = np.frexp(amax / 6.0)
    byte = np.clip(np.where(amax > 0, np.where(mant > 0.5, ex, ex - 1) + 127, 1), 1, 254)
    scaled = (w * np.exp2(127.0 - byte)[:, None, :]).reshape(k, n).astype(np.float32)
    c = np.ascontiguousarray(scaled.reshape(k // 512, 128, 4, n).transpose(0, 1, 3, 2)).astype(ml_dtypes.float4_e2m1fn).view(np.uint8) & 0xF
    words = (c[..., 0::2] | (c[..., 1::2] << 4)).reshape(k // 512, 128, 2 * n)
    return np.ascontiguousarray(words), np.ascontiguousarray(byte.astype(np.uint8).reshape(k // 512, 16, n))


def unpack_fp4(words, scales):
    g, _, n = scales.shape
    words = np.ascontiguousarray(words).reshape(g, 128, n, 2)
    nib = np.empty((g, 128, n, 4), np.uint8)
    nib[..., 0::2] = words & 0xF
    nib[..., 1::2] = words >> 4
    vals = E2M1[nib] * np.repeat(np.exp2(scales.astype(np.float64) - 127.0), 8, axis=1)[..., None]
    return vals.transpose(0, 1, 3, 2).reshape(g * 512, n)


def gelu(v):
    return 0.5 * v * (1.0 + np.tanh(np.sqrt(2.0 / np.pi) * (v + 0.044715 * v**3)))


K, T, S, H, N = 512, 2048, 1024, 512, 256
P = 2 ** 7


def setup_inputs():
    n = np.random.standard_normal
    s = mx_kscale(K)[:, None]
    u = mx_kscale(H)
    packed_w2 = pack_fp4(n((H, N)) / np.sqrt(H) / u[:, None])
    return {
        "xT": (n((K, T)) * s).astype(np.float32),
        "w1": (n((K, H)) / np.sqrt(K) / s * u).astype(np.float32),
        "w2_words": packed_w2[0],
        "w2_scales": packed_w2[1],
        "share": np.tile(np.random.uniform(0.1, 0.9, S), (P, 1)).astype(np.float32),
        "offs": striped(np.random.permutation(T)[:S]),
        "par": striped(np.random.permutation(S)[(S * np.random.uniform(0, 1, S) ** 4).astype(np.int64)]),
    }


def reference(xT, w1, w2_words, w2_scales, share, offs, par):
    xq = mxq(f64(xT)[:, unstriped(offs)], 0, "e4m3")
    h = gelu(mxq(f64(w1), 0, "e4m3").T @ xq)
    z = h + h[:, unstriped(par)] * f64(share)[:1]
    return unpack_fp4(w2_words, w2_scales).T @ mxq(z, 0, "e4m3")

@@ -1,0 +1,205 @@
+from contextlib import ExitStack
+
+import concourse.mybir as mybir
+from concourse.masks import make_identity
+
+K, T, S, H, N = 512, 2048, 1024, 512, 256
+FLOPS = 2 * K * H * S + 2 * H * N * S
+
+F32 = mybir.dt.float32
+BF16 = mybir.dt.bfloat16
+I32 = mybir.dt.int32
+U32 = mybir.dt.uint32
+U16 = mybir.dt.uint16
+U8 = mybir.dt.uint8
+FP8X4 = mybir.dt.float8_e4m3fn_x4
+FP4X4 = mybir.dt.float4_e2m1fn_x4
+GELU = mybir.ActivationFunctionType.Gelu_apprx_tanh
+MULT = mybir.AluOpType.mult
+ADD = mybir.AluOpType.add
+
+P = 128
+X0 = [512,512,512,512]
+X1 = [512,512,512,256,256]
+PICK = [512,256,256]
+PE_CH = [256,256,256]
+DIRECT = [256]
+
+
+def spans(widths, start=0):
+    res = []
+    for w in widths:
+        res.append((start, start + w))
+        start = start + w
+    return res
+
+
+def tile_picked_treeup_gelu_e_kernel(tc, xT, w1, w2_words, w2_scales, share, offs, par, out):
+    nc = tc.nc
+    with ExitStack() as ctx:
+        keep = ctx.enter_context(tc.tile_pool(name="keep", bufs=1))
+        psum = ctx.enter_context(tc.psum_pool(name="psum", bufs=1))
+
+        def bank(i):
+            return psum.tile([P, 512], F32, name="bank%d" % i)
+
+        offs_t = keep.tile([P, S // 16], U16, name="offs_t")
+        par_t = keep.tile([P, S // 16], U16, name="par_t")
+        nc.sync.dma_start(offs_t[:], offs)
+
+        warm = keep.tile([P, 8], F32, name="warm")
+        warm2 = keep.tile([P, 8], F32, name="warm2")
+        nc.gpsimd.memset(warm[:], 0.0)
+        nc.scalar.activation(out=warm2[:], in_=warm[:], func=GELU)
+
+        w2s = keep.tile([P, N], U8, name="w2s", align_bytes=64)
+        nc.gpsimd.memset(w2s[:].bitcast(I32), 0)
+        ident = keep.tile([P, P], F32, name="ident")
+        make_identity(nc, ident[:])
+
+        x4 = xT.rearrange("(p j) t -> p j t", j=4)
+        raw = {}
+        for u, widths in enumerate((X0, X1)):
+            for a, b in spans(widths):
+                raw[u, a] = keep.tile([P, 2, b - a], F32, name="raw%d_%d" % (u, a))
+                nc.sync.dma_start(raw[u, a][:], x4[:, 2 * u : 2 * u + 2, a:b])
+        w4 = w1.rearrange("(p j) c -> p j c", j=4)
+        wraw = []
+        for hh in range(2):
+            wraw.append(keep.tile([P, 4, 256], F32, name="wraw%d" % hh))
+            nc.sync.dma_start(wraw[hh][:], w4[:, :, 256 * hh : 256 * hh + 256])
+        nc.sync.dma_start(par_t[:], par)
+        share_t = {}
+        for a, b in spans(PE_CH + DIRECT):
+            share_t[a] = keep.tile([P, b - a], F32, name="share%d" % a)
+            nc.sync.dma_start(share_t[a][:], share[:, a:b])
+        w2w = keep.tile([P, 2 * N], U8, name="w2w", align_bytes=64)
+        nc.sync.dma_start(w2w[:], w2_words[0])
+        for q in range(4):
+            nc.sync.dma_start(w2s[32 * q : 32 * q + 4, :].bitcast(I32), w2_scales[0, 4 * q : 4 * q + 4, :].bitcast(I32))
+
+        pairs = [keep.tile([P, 2 * T], BF16, name="pairs%d" % u, align_bytes=64) for u in range(2)]
+
+        def cast(engine, u, a, b):
+            dst = pairs[u][:, 2 * a : 2 * b].rearrange("p (s e) -> p s e", e=2)
+            src = raw[u, a][:].rearrange("p e s -> p s e")
+            if engine == "v":
+                nc.vector.tensor_copy(out=dst, in_=src)
+            else:
+                nc.scalar.copy(out=dst, in_=src)
+
+        xg = {a: keep.tile([P, 4 * (b - a)], BF16, name="xg%d" % a, align_bytes=64) for a, b in spans(PICK)}
+        xq = {a: keep.tile([P, b - a], U32, name="xq%d" % a, align_bytes=64) for a, b in spans(PICK)}
+        xs = {a: keep.tile([P, b - a], U8, name="xs%d" % a, align_bytes=64) for a, b in spans(PICK)}
+
+        def pick(u, a, b):
+            dst = xg[a][:].bitcast(U32).rearrange("p (s u) -> p s u", u=2)[:, :, u]
+            nc.vector.tensor_copy(out=dst, in_=pairs[u][:].bitcast(U32).indirect(offs_t[:, a // 16 : b // 16]))
+
+        for a, b in spans(X0):
+            cast("v", 0, a, b)
+        for a, b in spans(PICK):
+            pick(0, a, b)
+        for a, b in spans(X1)[:-1]:
+            cast("s", 1, a, b)
+        cast("v", 1, spans(X1)[-1][0], T)
+
+        wg = keep.tile([P, 4 * H], BF16, name="wg", align_bytes=64)
+        wq = keep.tile([P, H], U32, name="wq", align_bytes=64)
+        ws = keep.tile([P, H], U8, name="ws", align_bytes=64)
+        for hh in range(2):
+            dst = wg[:].rearrange("p (t m j) -> p m j t", t=4, j=4)[:, 64 * hh : 64 * hh + 64, :, :]
+            nc.scalar.copy(out=dst, in_=wraw[hh][:].rearrange("p j (m t) -> p m j t", t=4))
+
+        def quant_w(t0, t1):
+            nc.vector.quantize_mx(out=wq[:, P * t0 : P * t1].bitcast(FP8X4), scales=ws[:, P * t0 : P * t1], in_=wg[:, 512 * t0 : 512 * t1])
+
+        picks = spans(PICK)
+        for i, (a, b) in enumerate(picks):
+            pick(1, a, b)
+            if i == len(picks) - 1:
+                quant_w(0, 1)
+            nc.vector.quantize_mx(out=xq[a][:].bitcast(FP8X4), scales=xs[a][:], in_=xg[a][:])
+        quant_w(1, 2)
+        quant_w(2, 4)
+
+        h = [keep.tile([P, S], F32, name="h%d" % t) for t in range(4)]
+        d0 = sum(PE_CH)
+        hd = keep.tile([P, 4, S - d0], F32, name="hd")
+        for t in range(4):
+            accs = [bank(2 * t), bank(2 * t + 1)]
+            for a, b in picks:
+                acc = accs[a // 512][:, a % 512 : a % 512 + b - a]
+                nc.tensor.matmul_mx(out=acc, lhsT=wq[:, P * t : P * t + P].bitcast(FP8X4), lhsT_scale=ws[:, P * t : P * t + P],
+                                    rhs=xq[a][:].bitcast(FP8X4), rhs_scale=xs[a][:], start=True, stop=True)
+                if b % 512 == 0:
+                    nc.scalar.activation(out=h[t][:, b - 512 : b], in_=accs[a // 512][:], func=GELU)
+            nc.sync.dma_start(hd[:, t, :], h[t][:, d0:S])
+
+        def follow(dst, t, a, b):
+            nc.vector.tensor_tensor(out=dst, in0=h[t][:].indirect(par_t[:, a // 16 : b // 16]), in1=share_t[a][:], op=MULT)
+
+        def finish(zg, a, b, last, obanks, engines):
+            n = b - a
+            zq = keep.tile([P, n], U32, name="zq%d" % a, align_bytes=64)
+            zs = keep.tile([P, n], U8, name="zs%d" % a, align_bytes=64)
+            nc.vector.quantize_mx(out=zq[:].bitcast(FP8X4), scales=zs[:], in_=zg)
+            for mb in range(2):
+                acc = bank(obanks[mb])
+                nc.tensor.matmul_mx(out=acc[:, 0:n], lhsT=w2w[:, 256 * mb : 256 * mb + 256].bitcast(FP4X4), lhsT_scale=w2s[:, P * mb : P * mb + P],
+                                    rhs=zq[:].bitcast(FP8X4), rhs_scale=zs[:], start=True, stop=True)
+                res = keep.tile([P, n], F32, name="res%d_%d" % (a, mb))
+                if engines[mb] == "v":
+                    nc.vector.tensor_copy(out=res[:], in_=acc[:, 0:n])
+                else:
+                    nc.scalar.copy(out=res[:], in_=acc[:, 0:n])
+                (nc.scalar if last and engines[mb] == "s" else nc.sync).dma_start(out[P * mb : P * mb + P, a:b], res[:])
+
+        def turn(banks, t, g, a):
+            for c, bk in enumerate(banks):
+                nc.tensor.matmul(out=bk[:, P * t : P * t + P], lhsT=h[t][:, a + P * c : a + P * c + P], rhs=ident[:], is_transpose=True, start=True, stop=False)
+            for c, bk in enumerate(banks):
+                nc.tensor.matmul(out=bk[:, P * t : P * t + P], lhsT=g[:, P * c : P * c + P], rhs=ident[:], is_transpose=True, start=False, stop=True)
+
+        def round_and_turn_back(banks, back, name):
+            for c, bk in enumerate(banks):
+                zt = keep.tile([P, 512], BF16, name="zt%s%d" % (name, c), align_bytes=64)
+                nc.scalar.copy(out=zt[:].rearrange("s (u p e) -> s u p e", u=2, e=2), in_=bk[:].rearrange("s (u e p) -> s u p e", u=2, e=2))
+                for u in range(2):
+                    col = 256 * c + P * u
+                    nc.tensor.transpose(back[:, col : col + P], zt[:].bitcast(F32)[:, P * u : P * u + P], ident[:])
+
+        def weave(dst, back):
+            nc.scalar.copy(out=dst.bitcast(F32).rearrange("p (c s u) -> p c s u", c=2, u=2), in_=back[:].rearrange("p (c u s) -> p c s u", c=2, u=2))
+
+        sums = {0: [bank(0), bank(1)], 256: [bank(2), bank(3)]}
+        for t in range(4):
+            for a in (0, 256):
+                g = keep.tile([P, 256], F32, name="g%d_%d" % (a, t))
+                follow(g[:], t, a, a + 256)
+                turn(sums[a], t, g[:], a)
+        zg_ab = keep.tile([P, 2048], BF16, name="zg_ab", align_bytes=64)
+        back_a, back_b = bank(4), bank(5)
+        round_and_turn_back(sums[0], back_a, "a")
+        round_and_turn_back(sums[256], back_b, "b")
+        weave(zg_ab[:, 0:1024], back_a)
+        weave(zg_ab[:, 1024:2048], back_b)
+        gc = keep.tile([P, 4, 256], F32, name="gc", tag="share0")
+        sums_c = [bank(0), bank(1)]
+        for t in range(4):
+            follow(gc[:, t, :], t, 512, 768)
+            turn(sums_c, t, gc[:, t, :], 512)
+        gd = keep.tile([P, 4, 256], F32, name="gd", tag="share256")
+        for t in range(4):
+            follow(gd[:, t, :], t, 768, 1024)
+        back_c = bank(2)
+        round_and_turn_back(sums_c, back_c, "c")
+        zg_c = keep.tile([P, 1024], BF16, name="zg_c", align_bytes=64)
+        weave(zg_c[:], back_c)
+        finish(zg_ab[:], 0, 512, False, [6, 7], "ss")
+        zg_d = keep.tile([P, 1024], BF16, name="zg_d", tag="ztc1", align_bytes=64)
+        nc.vector.tensor_tensor(out=zg_d[:].rearrange("p (c i t) -> p c t i", i=4, t=4),
+                                in0=gd[:].rearrange("p t (c i) -> p c t i", i=4),
+                                in1=hd[:].rearrange("p t (c i) -> p c t i", i=4), op=ADD)
+        finish(zg_c[:], 512, 768, False, [3, 4], "sv")
+        finish(zg_d[:], 768, 1024, True, [5, 0], "sv")

@@ -19,9 +19,9 @@ MULT = mybir.AluOpType.mult
 ADD = mybir.AluOpType.add
 
 P = 128
-X0 = [512,512,512,512]
+X0 = [1024,512,512]
 X1 = [512,512,512,256,256]
-PICK = [512,256,256]
+PICK = [512,512]
 PE_CH = [256,256,256]
 DIRECT = [256]
 
@@ -45,7 +45,6 @@ def tile_picked_treeup_gelu_e_kernel(tc, xT, w1, w2_words, w2_scales, share, off
 
         offs_t = keep.tile([P, S // 16], U16, name="offs_t")
         par_t = keep.tile([P, S // 16], U16, name="par_t")
-        nc.sync.dma_start(offs_t[:], offs)
 
         warm = keep.tile([P, 8], F32, name="warm")
         warm2 = keep.tile([P, 8], F32, name="warm2")
@@ -63,10 +62,12 @@ def tile_picked_treeup_gelu_e_kernel(tc, xT, w1, w2_words, w2_scales, share, off
             for a, b in spans(widths):
                 raw[u, a] = keep.tile([P, 2, b - a], F32, name="raw%d_%d" % (u, a))
                 nc.sync.dma_start(raw[u, a][:], x4[:, 2 * u : 2 * u + 2, a:b])
+                if (u, a) == (0, 0):
+                    nc.sync.dma_start(offs_t[:], offs)
         w4 = w1.rearrange("(p j) c -> p j c", j=4)
         wraw = []
         for hh in range(2):
-            wraw.append(keep.tile([P, 4, 256], F32, name="wraw%d" % hh))
+            wraw.append(keep.tile([P, 4, 256], F32, name="wraw%d" % hh, align_bytes=64))
             nc.sync.dma_start(wraw[hh][:], w4[:, :, 256 * hh : 256 * hh + 256])
         nc.sync.dma_start(par_t[:], par)
         share_t = {}
@@ -89,8 +90,6 @@ def tile_picked_treeup_gelu_e_kernel(tc, xT, w1, w2_words, w2_scales, share, off
                 nc.scalar.copy(out=dst, in_=src)
 
         xg = {a: keep.tile([P, 4 * (b - a)], BF16, name="xg%d" % a, align_bytes=64) for a, b in spans(PICK)}
-        xq = {a: keep.tile([P, b - a], U32, name="xq%d" % a, align_bytes=64) for a, b in spans(PICK)}
-        xs = {a: keep.tile([P, b - a], U8, name="xs%d" % a, align_bytes=64) for a, b in spans(PICK)}
 
         def pick(u, a, b):
             dst = xg[a][:].bitcast(U32).rearrange("p (s u) -> p s u", u=2)[:, :, u]
@@ -100,40 +99,58 @@ def tile_picked_treeup_gelu_e_kernel(tc, xT, w1, w2_words, w2_scales, share, off
             cast("v", 0, a, b)
         for a, b in spans(PICK):
             pick(0, a, b)
-        for a, b in spans(X1)[:-1]:
+        for a, b in spans(X1)[:-2]:
             cast("s", 1, a, b)
-        cast("v", 1, spans(X1)[-1][0], T)
+        for a, b in spans(X1)[-2:]:
+            cast("v", 1, a, b)
 
         wg = keep.tile([P, 4 * H], BF16, name="wg", align_bytes=64)
-        wq = keep.tile([P, H], U32, name="wq", align_bytes=64)
-        ws = keep.tile([P, H], U8, name="ws", align_bytes=64)
         for hh in range(2):
             dst = wg[:].rearrange("p (t m j) -> p m j t", t=4, j=4)[:, 64 * hh : 64 * hh + 64, :, :]
             nc.scalar.copy(out=dst, in_=wraw[hh][:].rearrange("p j (m t) -> p m j t", t=4))
 
-        def quant_w(t0, t1):
-            nc.vector.quantize_mx(out=wq[:, P * t0 : P * t1].bitcast(FP8X4), scales=ws[:, P * t0 : P * t1], in_=wg[:, 512 * t0 : 512 * t1])
-
         picks = spans(PICK)
-        for i, (a, b) in enumerate(picks):
+        for a, b in picks:
             pick(1, a, b)
-            if i == len(picks) - 1:
-                quant_w(0, 1)
-            nc.vector.quantize_mx(out=xq[a][:].bitcast(FP8X4), scales=xs[a][:], in_=xg[a][:])
-        quant_w(1, 2)
-        quant_w(2, 4)
+        E = 256
+        xs = keep.tile([P, S], U8, name="xs", align_bytes=64)
+        xq_early = keep.tile([P, E], U32, name="xq_early", align_bytes=64)
+        xq_late = keep.tile([P, S - E], U32, name="xq_late", tag="wraw1", align_bytes=64)
+        ws = keep.tile([P, H], U8, name="ws", align_bytes=64)
+        wq_first = keep.tile([P, P], U32, name="wq_first", align_bytes=64)
+
+        def xq(a, b):
+            return (xq_early[:, a:b] if b <= E else xq_late[:, a - E : b - E]).bitcast(FP8X4)
+
+        def quant_x(a):
+            nc.vector.quantize_mx(out=xq(a, a + 256), scales=xs[:, a : a + 256], in_=xg[a // 512 * 512][:, 4 * (a % 512) : 4 * (a % 512) + 1024])
+
+        for a in range(0, E, 256):
+            quant_x(a)
+        nc.vector.quantize_mx(out=wq_first[:].bitcast(FP8X4), scales=ws[:, 0:P], in_=wg[:, 0:512])
+        for a in range(E, S, 256):
+            quant_x(a)
+        wq_rest = keep.tile([P, 3 * P], U32, name="wq_rest", align_bytes=64)
+        nc.vector.quantize_mx(out=wq_rest[:, 0:P].bitcast(FP8X4), scales=ws[:, P : 2 * P], in_=wg[:, 512:1024])
+        nc.vector.quantize_mx(out=wq_rest[:, P : 3 * P].bitcast(FP8X4), scales=ws[:, 2 * P : 4 * P], in_=wg[:, 1024:2048])
 
         h = [keep.tile([P, S], F32, name="h%d" % t) for t in range(4)]
         d0 = sum(PE_CH)
         hd = keep.tile([P, 4, S - d0], F32, name="hd")
         for t in range(4):
-            accs = [bank(2 * t), bank(2 * t + 1)]
-            for a, b in picks:
-                acc = accs[a // 512][:, a % 512 : a % 512 + b - a]
-                nc.tensor.matmul_mx(out=acc, lhsT=wq[:, P * t : P * t + P].bitcast(FP8X4), lhsT_scale=ws[:, P * t : P * t + P],
-                                    rhs=xq[a][:].bitcast(FP8X4), rhs_scale=xs[a][:], start=True, stop=True)
-                if b % 512 == 0:
-                    nc.scalar.activation(out=h[t][:, b - 512 : b], in_=accs[a // 512][:], func=GELU)
+            wq = (wq_first[:] if t == 0 else wq_rest[:, P * (t - 1) : P * t]).bitcast(FP8X4)
+            if t == 0:
+                for a, i in zip(range(0, S, 256), (0, 1, 6, 7)):
+                    acc = bank(i)[:, 0:256]
+                    nc.tensor.matmul_mx(out=acc, lhsT=wq, lhsT_scale=ws[:, 0:P], rhs=xq(a, a + 256), rhs_scale=xs[:, a : a + 256], start=True, stop=True)
+                    nc.scalar.activation(out=h[0][:, a : a + 256], in_=acc, func=GELU)
+            else:
+                accs = [bank(2 * t), bank(2 * t + 1)]
+                for a, b in spans([256, 256, 512] if E == 256 else [512, 512]):
+                    nc.tensor.matmul_mx(out=accs[a // 512][:, a % 512 : a % 512 + b - a], lhsT=wq, lhsT_scale=ws[:, P * t : P * t + P],
+                                        rhs=xq(a, b), rhs_scale=xs[:, a:b], start=True, stop=True)
+                    if b % 512 == 0:
+                        nc.scalar.activation(out=h[t][:, b - 512 : b], in_=accs[a // 512][:], func=GELU)
             nc.sync.dma_start(hd[:, t, :], h[t][:, d0:S])
 
         def follow(dst, t, a, b):
@@ -161,16 +178,15 @@ def tile_picked_treeup_gelu_e_kernel(tc, xT, w1, w2_words, w2_scales, share, off
             for c, bk in enumerate(banks):
                 nc.tensor.matmul(out=bk[:, P * t : P * t + P], lhsT=g[:, P * c : P * c + P], rhs=ident[:], is_transpose=True, start=False, stop=True)
 
-        def round_and_turn_back(banks, back, name):
+        def round_and_turn_back(banks, backs, name):
             for c, bk in enumerate(banks):
                 zt = keep.tile([P, 512], BF16, name="zt%s%d" % (name, c), align_bytes=64)
                 nc.scalar.copy(out=zt[:].rearrange("s (u p e) -> s u p e", u=2, e=2), in_=bk[:].rearrange("s (u e p) -> s u p e", u=2, e=2))
                 for u in range(2):
-                    col = 256 * c + P * u
-                    nc.tensor.transpose(back[:, col : col + P], zt[:].bitcast(F32)[:, P * u : P * u + P], ident[:])
+                    nc.tensor.transpose(backs[c][:, P * u : P * u + P], zt[:].bitcast(F32)[:, P * u : P * u + P], ident[:])
 
-        def weave(dst, back):
-            nc.scalar.copy(out=dst.bitcast(F32).rearrange("p (c s u) -> p c s u", c=2, u=2), in_=back[:].rearrange("p (c u s) -> p c s u", c=2, u=2))
+        def weave(dst, back, blocks):
+            nc.scalar.copy(out=dst.bitcast(F32).rearrange("p (c s u) -> p c s u", c=blocks, u=2), in_=back.rearrange("p (c u s) -> p c s u", c=blocks, u=2))
 
         sums = {0: [bank(0), bank(1)], 256: [bank(2), bank(3)]}
         for t in range(4):
@@ -180,10 +196,10 @@ def tile_picked_treeup_gelu_e_kernel(tc, xT, w1, w2_words, w2_scales, share, off
                 turn(sums[a], t, g[:], a)
         zg_ab = keep.tile([P, 2048], BF16, name="zg_ab", align_bytes=64)
         back_a, back_b = bank(4), bank(5)
-        round_and_turn_back(sums[0], back_a, "a")
-        round_and_turn_back(sums[256], back_b, "b")
-        weave(zg_ab[:, 0:1024], back_a)
-        weave(zg_ab[:, 1024:2048], back_b)
+        round_and_turn_back(sums[0], [back_a[:, 0:256], back_a[:, 256:512]], "a")
+        round_and_turn_back(sums[256], [back_b[:, 0:256], back_b[:, 256:512]], "b")
+        weave(zg_ab[:, 0:1024], back_a[:], 2)
+        weave(zg_ab[:, 1024:2048], back_b[:], 2)
         gc = keep.tile([P, 4, 256], F32, name="gc", tag="share0")
         sums_c = [bank(0), bank(1)]
         for t in range(4):
@@ -192,14 +208,17 @@ def tile_picked_treeup_gelu_e_kernel(tc, xT, w1, w2_words, w2_scales, share, off
         gd = keep.tile([P, 4, 256], F32, name="gd", tag="share256")
         for t in range(4):
             follow(gd[:, t, :], t, 768, 1024)
-        back_c = bank(2)
+        back_c = [bank(2)[:, 0:256], bank(3)[:, 0:256]]
         round_and_turn_back(sums_c, back_c, "c")
         zg_c = keep.tile([P, 1024], BF16, name="zg_c", align_bytes=64)
-        weave(zg_c[:], back_c)
-        finish(zg_ab[:], 0, 512, False, [6, 7], "ss")
+        for c in range(2):
+            weave(zg_c[:, 512 * c : 512 * c + 512], back_c[c], 1)
+        finish(zg_ab[:], 0, 512, False, [2, 3], "ss")
         zg_d = keep.tile([P, 1024], BF16, name="zg_d", tag="ztc1", align_bytes=64)
-        nc.vector.tensor_tensor(out=zg_d[:].rearrange("p (c i t) -> p c t i", i=4, t=4),
-                                in0=gd[:].rearrange("p t (c i) -> p c t i", i=4),
-                                in1=hd[:].rearrange("p t (c i) -> p c t i", i=4), op=ADD)
-        finish(zg_c[:], 512, 768, False, [3, 4], "sv")
-        finish(zg_d[:], 768, 1024, True, [5, 0], "sv")
+        for a in (0, 128):
+            nc.vector.tensor_tensor(out=zg_d[:, 4 * a : 4 * a + 512].rearrange("p (c i t) -> p c t i", i=4, t=4),
+                                    in0=gd[:, :, a : a + P].rearrange("p t (c i) -> p c t i", i=4),
+                                    in1=hd[:, :, a : a + P].rearrange("p t (c i) -> p c t i", i=4), op=ADD)
+        finish(zg_c[:], 512, 768, False, [6, 7], "ss")
+        finish(zg_d[:, 0:512], 768, 896, False, [4, 5], "sv")
+        finish(zg_d[:, 512:1024], 896, 1024, True, [0, 1], "sv")

@@ -19,11 +19,11 @@ MULT = mybir.AluOpType.mult
 ADD = mybir.AluOpType.add
 
 P = 128
-X0 = [1024,512,512]
-X1 = [512,512,512,256,256]
+X0 = [1024,1024]
+X1 = [1024,512,512]
 PICK = [512,512]
-PE_CH = [256,256,256]
-DIRECT = [256]
+PE_CH = [256,256]
+DIRECT = [256,256]
 
 
 def spans(widths, start=0):
@@ -70,10 +70,8 @@ def tile_picked_treeup_gelu_e_kernel(tc, xT, w1, w2_words, w2_scales, share, off
             wraw.append(keep.tile([P, 4, 256], F32, name="wraw%d" % hh, align_bytes=64))
             nc.sync.dma_start(wraw[hh][:], w4[:, :, 256 * hh : 256 * hh + 256])
         nc.sync.dma_start(par_t[:], par)
-        share_t = {}
-        for a, b in spans(PE_CH + DIRECT):
-            share_t[a] = keep.tile([P, b - a], F32, name="share%d" % a)
-            nc.sync.dma_start(share_t[a][:], share[:, a:b])
+        share_t = keep.tile([P, S], F32, name="share_t")
+        nc.sync.dma_start(share_t[:], share)
         w2w = keep.tile([P, 2 * N], U8, name="w2w", align_bytes=64)
         nc.sync.dma_start(w2w[:], w2_words[0])
         for q in range(4):
@@ -81,9 +79,9 @@ def tile_picked_treeup_gelu_e_kernel(tc, xT, w1, w2_words, w2_scales, share, off
 
         pairs = [keep.tile([P, 2 * T], BF16, name="pairs%d" % u, align_bytes=64) for u in range(2)]
 
-        def cast(engine, u, a, b):
+        def cast(engine, u, first, a, b):
             dst = pairs[u][:, 2 * a : 2 * b].rearrange("p (s e) -> p s e", e=2)
-            src = raw[u, a][:].rearrange("p e s -> p s e")
+            src = raw[u, first][:, :, a - first : b - first].rearrange("p e s -> p s e")
             if engine == "v":
                 nc.vector.tensor_copy(out=dst, in_=src)
             else:
@@ -95,14 +93,15 @@ def tile_picked_treeup_gelu_e_kernel(tc, xT, w1, w2_words, w2_scales, share, off
             dst = xg[a][:].bitcast(U32).rearrange("p (s u) -> p s u", u=2)[:, :, u]
             nc.vector.tensor_copy(out=dst, in_=pairs[u][:].bitcast(U32).indirect(offs_t[:, a // 16 : b // 16]))
 
-        for a, b in spans(X0):
-            cast("v", 0, a, b)
+        cast("v", 0, 0, 0, 1024)
+        cast("v", 0, 1024, 1024, 1728)
+        cast("s", 0, 1024, 1728, 2048)
         for a, b in spans(PICK):
             pick(0, a, b)
-        for a, b in spans(X1)[:-2]:
-            cast("s", 1, a, b)
-        for a, b in spans(X1)[-2:]:
-            cast("v", 1, a, b)
+        cast("s", 1, 0, 0, 1024)
+        cast("v", 1, 1024, 1024, 1536)
+        cast("v", 1, 1536, 1536, 1888)
+        cast("s", 1, 1536, 1888, 2048)
 
         wg = keep.tile([P, 4 * H], BF16, name="wg", align_bytes=64)
         for hh in range(2):
@@ -154,7 +153,7 @@ def tile_picked_treeup_gelu_e_kernel(tc, xT, w1, w2_words, w2_scales, share, off
             nc.sync.dma_start(hd[:, t, :], h[t][:, d0:S])
 
         def follow(dst, t, a, b):
-            nc.vector.tensor_tensor(out=dst, in0=h[t][:].indirect(par_t[:, a // 16 : b // 16]), in1=share_t[a][:], op=MULT)
+            nc.vector.tensor_tensor(out=dst, in0=h[t][:].indirect(par_t[:, a // 16 : b // 16]), in1=share_t[:, a:b], op=MULT)
 
         def finish(zg, a, b, last, obanks, engines):
             n = b - a
@@ -188,37 +187,36 @@ def tile_picked_treeup_gelu_e_kernel(tc, xT, w1, w2_words, w2_scales, share, off
         def weave(dst, back, blocks):
             nc.scalar.copy(out=dst.bitcast(F32).rearrange("p (c s u) -> p c s u", c=blocks, u=2), in_=back.rearrange("p (c u s) -> p c s u", c=blocks, u=2))
 
-        sums = {0: [bank(0), bank(1)], 256: [bank(2), bank(3)]}
-        for t in range(4):
-            for a in (0, 256):
-                g = keep.tile([P, 256], F32, name="g%d_%d" % (a, t))
-                follow(g[:], t, a, a + 256)
-                turn(sums[a], t, g[:], a)
-        zg_ab = keep.tile([P, 2048], BF16, name="zg_ab", align_bytes=64)
-        back_a, back_b = bank(4), bank(5)
-        round_and_turn_back(sums[0], [back_a[:, 0:256], back_a[:, 256:512]], "a")
-        round_and_turn_back(sums[256], [back_b[:, 0:256], back_b[:, 256:512]], "b")
-        weave(zg_ab[:, 0:1024], back_a[:], 2)
-        weave(zg_ab[:, 1024:2048], back_b[:], 2)
-        gc = keep.tile([P, 4, 256], F32, name="gc", tag="share0")
-        sums_c = [bank(0), bank(1)]
+        sums = [bank(0), bank(1), bank(2), bank(3)]
+        for t in range(3):
+            g = keep.tile([P, 512], F32, name="g%d" % t)
+            follow(g[:], t, 0, 512)
+            turn(sums, t, g[:], 0)
+        for a in (0, 256):
+            g = keep.tile([P, 256], F32, name="g3_%d" % a)
+            follow(g[:], 3, a, a + 256)
+            turn(sums[a // P : a // P + 2], 3, g[:], a)
+        gc = keep.tile([P, 4, 256], F32, name="gc", tag="g2")
         for t in range(4):
             follow(gc[:, t, :], t, 512, 768)
-            turn(sums_c, t, gc[:, t, :], 512)
-        gd = keep.tile([P, 4, 256], F32, name="gd", tag="share256")
+        zg_c = keep.tile([P, 1024], BF16, name="zg_c", align_bytes=64)
+        nc.vector.tensor_tensor(out=zg_c[:].rearrange("p (c i t) -> p c t i", i=4, t=4),
+                                    in0=gc[:].rearrange("p t (c i) -> p c t i", i=4),
+                                    in1=hd[:, :, 0:256].rearrange("p t (c i) -> p c t i", i=4), op=ADD)
+        for a, name in ((0, "a"), (256, "b")):
+            back = bank(4 + a // 256)
+            round_and_turn_back(sums[a // P : a // P + 2], [back[:, 0:256], back[:, 256:512]], name)
+            zg = keep.tile([P, 1024], BF16, name="zg_" + name, align_bytes=64)
+            weave(zg[:], back[:], 2)
+            finish(zg[:], a, a + 256, False, [6, 7] if a == 0 else [2, 3], "ss")
+        finish(zg_c[:], 512, 768, False, [0, 1], "ss")
+        gd = keep.tile([P, 4, 256], F32, name="gd", tag="g2")
         for t in range(4):
             follow(gd[:, t, :], t, 768, 1024)
-        back_c = [bank(2)[:, 0:256], bank(3)[:, 0:256]]
-        round_and_turn_back(sums_c, back_c, "c")
-        zg_c = keep.tile([P, 1024], BF16, name="zg_c", align_bytes=64)
-        for c in range(2):
-            weave(zg_c[:, 512 * c : 512 * c + 512], back_c[c], 1)
-        finish(zg_ab[:], 0, 512, False, [2, 3], "ss")
-        zg_d = keep.tile([P, 1024], BF16, name="zg_d", tag="ztc1", align_bytes=64)
+        zg_d = keep.tile([P, 1024], BF16, name="zg_d", align_bytes=64)
         for a in (0, 128):
             nc.vector.tensor_tensor(out=zg_d[:, 4 * a : 4 * a + 512].rearrange("p (c i t) -> p c t i", i=4, t=4),
                                     in0=gd[:, :, a : a + P].rearrange("p t (c i) -> p c t i", i=4),
-                                    in1=hd[:, :, a : a + P].rearrange("p t (c i) -> p c t i", i=4), op=ADD)
-        finish(zg_c[:], 512, 768, False, [6, 7], "ss")
-        finish(zg_d[:, 0:512], 768, 896, False, [4, 5], "sv")
-        finish(zg_d[:, 512:1024], 896, 1024, True, [0, 1], "sv")
+                                    in1=hd[:, :, 256 + a : 256 + a + P].rearrange("p t (c i) -> p c t i", i=4), op=ADD)
+        finish(zg_d[:, 0:512], 768, 896, False, [4, 5], "ss")
+        finish(zg_d[:, 512:1024], 896, 1024, True, [6, 7], "sv")

@@ -46,11 +46,6 @@ def tile_picked_treeup_gelu_e_kernel(tc, xT, w1, w2_words, w2_scales, share, off
         offs_t = keep.tile([P, S // 16], U16, name="offs_t")
         par_t = keep.tile([P, S // 16], U16, name="par_t")
 
-        warm = keep.tile([P, 8], F32, name="warm")
-        warm2 = keep.tile([P, 8], F32, name="warm2")
-        nc.gpsimd.memset(warm[:], 0.0)
-        nc.scalar.activation(out=warm2[:], in_=warm[:], func=GELU)
-
         w2s = keep.tile([P, N], U8, name="w2s", align_bytes=64)
         nc.gpsimd.memset(w2s[:].bitcast(I32), 0)
         ident = keep.tile([P, P], F32, name="ident")
@@ -133,9 +128,10 @@ def tile_picked_treeup_gelu_e_kernel(tc, xT, w1, w2_words, w2_scales, share, off
         nc.vector.quantize_mx(out=wq_rest[:, 0:P].bitcast(FP8X4), scales=ws[:, P : 2 * P], in_=wg[:, 512:1024])
         nc.vector.quantize_mx(out=wq_rest[:, P : 3 * P].bitcast(FP8X4), scales=ws[:, 2 * P : 4 * P], in_=wg[:, 1024:2048])
 
-        h = [keep.tile([P, S], F32, name="h%d" % t) for t in range(4)]
+        h = [keep.tile([P, S], F32, name="h%d" % t, align_bytes=64) for t in range(4)]
         d0 = sum(PE_CH)
-        hd = keep.tile([P, 4, S - d0], F32, name="hd")
+        hc = keep.tile([P, 4, P], F32, name="hc")
+        hd = keep.tile([P, 4, 384], F32, name="hd")
         for t in range(4):
             wq = (wq_first[:] if t == 0 else wq_rest[:, P * (t - 1) : P * t]).bitcast(FP8X4)
             if t == 0:
@@ -150,14 +146,15 @@ def tile_picked_treeup_gelu_e_kernel(tc, xT, w1, w2_words, w2_scales, share, off
                                         rhs=xq(a, b), rhs_scale=xs[:, a:b], start=True, stop=True)
                     if b % 512 == 0:
                         nc.scalar.activation(out=h[t][:, b - 512 : b], in_=accs[a // 512][:], func=GELU)
-            nc.sync.dma_start(hd[:, t, :], h[t][:, d0:S])
+            nc.sync.dma_start(hc[:, t, :], h[t][:, 512:640])
+            nc.sync.dma_start(hd[:, t, :], h[t][:, 640:S])
 
         def follow(dst, t, a, b):
             nc.vector.tensor_tensor(out=dst, in0=h[t][:].indirect(par_t[:, a // 16 : b // 16]), in1=share_t[:, a:b], op=MULT)
 
-        def finish(zg, a, b, last, obanks, engines):
+        def finish(zg, a, b, last, obanks, engines, slot=None):
             n = b - a
-            zq = keep.tile([P, n], U32, name="zq%d" % a, align_bytes=64)
+            zq = keep.tile([P, n], U32, name="zq%d" % a, tag=slot or "zq%d" % a, align_bytes=64)
             zs = keep.tile([P, n], U8, name="zs%d" % a, align_bytes=64)
             nc.vector.quantize_mx(out=zq[:].bitcast(FP8X4), scales=zs[:], in_=zg)
             for mb in range(2):
@@ -200,23 +197,24 @@ def tile_picked_treeup_gelu_e_kernel(tc, xT, w1, w2_words, w2_scales, share, off
         for t in range(4):
             follow(gc[:, t, :], t, 512, 768)
         zg_c = keep.tile([P, 1024], BF16, name="zg_c", align_bytes=64)
-        nc.vector.tensor_tensor(out=zg_c[:].rearrange("p (c i t) -> p c t i", i=4, t=4),
-                                    in0=gc[:].rearrange("p t (c i) -> p c t i", i=4),
-                                    in1=hd[:, :, 0:256].rearrange("p t (c i) -> p c t i", i=4), op=ADD)
+        for a, hh in ((0, hc[:]), (P, hd[:, :, 0:P])):
+            nc.vector.tensor_tensor(out=zg_c[:, 4 * a : 4 * a + 512].rearrange("p (c i t) -> p c t i", i=4, t=4),
+                                    in0=gc[:, :, a : a + P].rearrange("p t (c i) -> p c t i", i=4),
+                                    in1=hh.rearrange("p t (c i) -> p c t i", i=4), op=ADD)
+        finish(zg_c[:], 512, 768, False, [6, 7], "ss")
+        gd = keep.tile([P, 4, 256], F32, name="gd", tag="hc")
+        for t in range(4):
+            follow(gd[:, t, :], t, 768, 1024)
         for a, name in ((0, "a"), (256, "b")):
             back = bank(4 + a // 256)
             round_and_turn_back(sums[a // P : a // P + 2], [back[:, 0:256], back[:, 256:512]], name)
             zg = keep.tile([P, 1024], BF16, name="zg_" + name, align_bytes=64)
             weave(zg[:], back[:], 2)
-            finish(zg[:], a, a + 256, False, [6, 7] if a == 0 else [2, 3], "ss")
-        finish(zg_c[:], 512, 768, False, [0, 1], "ss")
-        gd = keep.tile([P, 4, 256], F32, name="gd", tag="g2")
-        for t in range(4):
-            follow(gd[:, t, :], t, 768, 1024)
+            finish(zg[:], a, a + 256, False, [0, 1] if a == 0 else [2, 3], "ss", "h%d" % (1 + a // 256))
         zg_d = keep.tile([P, 1024], BF16, name="zg_d", align_bytes=64)
         for a in (0, 128):
             nc.vector.tensor_tensor(out=zg_d[:, 4 * a : 4 * a + 512].rearrange("p (c i t) -> p c t i", i=4, t=4),
                                     in0=gd[:, :, a : a + P].rearrange("p t (c i) -> p c t i", i=4),
-                                    in1=hd[:, :, 256 + a : 256 + a + P].rearrange("p t (c i) -> p c t i", i=4), op=ADD)
+                                    in1=hd[:, :, P + a : 2 * P + a].rearrange("p t (c i) -> p c t i", i=4), op=ADD)
         finish(zg_d[:, 0:512], 768, 896, False, [4, 5], "ss")
         finish(zg_d[:, 512:1024], 896, 1024, True, [6, 7], "sv")

@@ -19,7 +19,7 @@ MULT = mybir.AluOpType.mult
 ADD = mybir.AluOpType.add
 
 P = 128
-X0 = [1024,1024]
+X0 = [1024,512,512]
 X1 = [1024,512,512]
 PICK = [512,512]
 PE_CH = [256,256]
@@ -48,6 +48,8 @@ def tile_picked_treeup_gelu_e_kernel(tc, xT, w1, w2_words, w2_scales, share, off
 
         w2s = keep.tile([P, N], U8, name="w2s", align_bytes=64)
         nc.gpsimd.memset(w2s[:].bitcast(I32), 0)
+        warm = keep.tile([P, 1], F32, name="warm")
+        nc.scalar.activation(out=warm[:], in_=w2s[:].bitcast(F32)[:, 0:1], func=GELU)
         ident = keep.tile([P, P], F32, name="ident")
         make_identity(nc, ident[:])
 
@@ -89,8 +91,9 @@ def tile_picked_treeup_gelu_e_kernel(tc, xT, w1, w2_words, w2_scales, share, off
             nc.vector.tensor_copy(out=dst, in_=pairs[u][:].bitcast(U32).indirect(offs_t[:, a // 16 : b // 16]))
 
         cast("v", 0, 0, 0, 1024)
-        cast("v", 0, 1024, 1024, 1728)
-        cast("s", 0, 1024, 1728, 2048)
+        cast("s", 0, 1024, 1024, 1536)
+        cast("v", 0, 1536, 1536, 1888)
+        cast("s", 0, 1536, 1888, 2048)
         for a, b in spans(PICK):
             pick(0, a, b)
         cast("s", 1, 0, 0, 1024)
@@ -106,7 +109,7 @@ def tile_picked_treeup_gelu_e_kernel(tc, xT, w1, w2_words, w2_scales, share, off
         picks = spans(PICK)
         for a, b in picks:
             pick(1, a, b)
-        E = 256
+        E = 512
         xs = keep.tile([P, S], U8, name="xs", align_bytes=64)
         xq_early = keep.tile([P, E], U32, name="xq_early", align_bytes=64)
         xq_late = keep.tile([P, S - E], U32, name="xq_late", tag="wraw1", align_bytes=64)
@@ -130,18 +133,21 @@ def tile_picked_treeup_gelu_e_kernel(tc, xT, w1, w2_words, w2_scales, share, off
 
         h = [keep.tile([P, S], F32, name="h%d" % t, align_bytes=64) for t in range(4)]
         d0 = sum(PE_CH)
-        hc = keep.tile([P, 4, P], F32, name="hc")
+        turns = keep.tile([P, 1792], F32, name="turns", align_bytes=64)
+        hc = turns[:, 0:768].rearrange("p (t s) -> p t s", t=4)[:, :, 0:P]
+        gd = turns[:, 0:1024].rearrange("p (t s) -> p t s", t=4)
+        zg_ab = turns[:, 768:1792].bitcast(BF16)
         hd = keep.tile([P, 4, 384], F32, name="hd")
         for t in range(4):
             wq = (wq_first[:] if t == 0 else wq_rest[:, P * (t - 1) : P * t]).bitcast(FP8X4)
             if t == 0:
-                for a, i in zip(range(0, S, 256), (0, 1, 6, 7)):
-                    acc = bank(i)[:, 0:256]
-                    nc.tensor.matmul_mx(out=acc, lhsT=wq, lhsT_scale=ws[:, 0:P], rhs=xq(a, a + 256), rhs_scale=xs[:, a : a + 256], start=True, stop=True)
-                    nc.scalar.activation(out=h[0][:, a : a + 256], in_=acc, func=GELU)
+                for (a, b), i in zip(spans([512, 256, 256]), (0, 6, 7)):
+                    acc = bank(i)[:, 0 : b - a]
+                    nc.tensor.matmul_mx(out=acc, lhsT=wq, lhsT_scale=ws[:, 0:P], rhs=xq(a, b), rhs_scale=xs[:, a:b], start=True, stop=True)
+                    nc.scalar.activation(out=h[0][:, a:b], in_=acc, func=GELU)
             else:
                 accs = [bank(2 * t), bank(2 * t + 1)]
-                for a, b in spans([256, 256, 512] if E == 256 else [512, 512]):
+                for a, b in spans([512, 512]):
                     nc.tensor.matmul_mx(out=accs[a // 512][:, a % 512 : a % 512 + b - a], lhsT=wq, lhsT_scale=ws[:, P * t : P * t + P],
                                         rhs=xq(a, b), rhs_scale=xs[:, a:b], start=True, stop=True)
                     if b % 512 == 0:
@@ -185,36 +191,32 @@ def tile_picked_treeup_gelu_e_kernel(tc, xT, w1, w2_words, w2_scales, share, off
             nc.scalar.copy(out=dst.bitcast(F32).rearrange("p (c s u) -> p c s u", c=blocks, u=2), in_=back.rearrange("p (c u s) -> p c s u", c=blocks, u=2))
 
         sums = [bank(0), bank(1), bank(2), bank(3)]
+        g = keep.tile([P, 4, 768], F32, name="g")
         for t in range(3):
-            g = keep.tile([P, 512], F32, name="g%d" % t)
-            follow(g[:], t, 0, 512)
-            turn(sums, t, g[:], 0)
-        for a in (0, 256):
-            g = keep.tile([P, 256], F32, name="g3_%d" % a)
-            follow(g[:], 3, a, a + 256)
-            turn(sums[a // P : a // P + 2], 3, g[:], a)
-        gc = keep.tile([P, 4, 256], F32, name="gc", tag="g2")
-        for t in range(4):
-            follow(gc[:, t, :], t, 512, 768)
+            follow(g[:, t, :], t, 0, 768)
+            turn(sums, t, g[:, t, :], 0)
+        for a in (0, 256, 512):
+            follow(g[:, 3, a : a + 256], 3, a, a + 256)
+            if a < 512:
+                turn(sums[a // P : a // P + 2], 3, g[:, 3, a : a + 256], a)
         zg_c = keep.tile([P, 1024], BF16, name="zg_c", align_bytes=64)
-        for a, hh in ((0, hc[:]), (P, hd[:, :, 0:P])):
+        for a, hh in ((0, hc), (P, hd[:, :, 0:P])):
             nc.vector.tensor_tensor(out=zg_c[:, 4 * a : 4 * a + 512].rearrange("p (c i t) -> p c t i", i=4, t=4),
-                                    in0=gc[:, :, a : a + P].rearrange("p t (c i) -> p c t i", i=4),
+                                    in0=g[:, :, 512 + a : 512 + a + P].rearrange("p t (c i) -> p c t i", i=4),
                                     in1=hh.rearrange("p t (c i) -> p c t i", i=4), op=ADD)
         finish(zg_c[:], 512, 768, False, [6, 7], "ss")
-        gd = keep.tile([P, 4, 256], F32, name="gd", tag="hc")
-        for t in range(4):
-            follow(gd[:, t, :], t, 768, 1024)
         for a, name in ((0, "a"), (256, "b")):
             back = bank(4 + a // 256)
             round_and_turn_back(sums[a // P : a // P + 2], [back[:, 0:256], back[:, 256:512]], name)
-            zg = keep.tile([P, 1024], BF16, name="zg_" + name, align_bytes=64)
-            weave(zg[:], back[:], 2)
-            finish(zg[:], a, a + 256, False, [0, 1] if a == 0 else [2, 3], "ss", "h%d" % (1 + a // 256))
+            weave(zg_ab[:, 4 * a : 4 * a + 1024], back[:], 2)
+        for t in range(3):
+            follow(gd[:, t, :], t, 768, 1024)
+        finish(zg_ab, 0, 512, False, [0, 1], "ss")
+        follow(gd[:, 3, :], 3, 768, 1024)
         zg_d = keep.tile([P, 1024], BF16, name="zg_d", align_bytes=64)
         for a in (0, 128):
             nc.vector.tensor_tensor(out=zg_d[:, 4 * a : 4 * a + 512].rearrange("p (c i t) -> p c t i", i=4, t=4),
                                     in0=gd[:, :, a : a + P].rearrange("p t (c i) -> p c t i", i=4),
                                     in1=hd[:, :, P + a : 2 * P + a].rearrange("p t (c i) -> p c t i", i=4), op=ADD)
-        finish(zg_d[:, 0:512], 768, 896, False, [4, 5], "ss")
-        finish(zg_d[:, 512:1024], 896, 1024, True, [6, 7], "sv")
+        finish(zg_d[:, 0:512], 768, 896, False, [2, 3], "ss")
+        finish(zg_d[:, 512:1024], 896, 1024, True, [4, 5], "sv")

@@ -20,7 +20,7 @@ ADD = mybir.AluOpType.add
 
 P = 128
 X0 = [1024,512,512]
-X1 = [1024,512,512]
+X1 = [768,768,256,256]
 PICK = [512,512]
 PE_CH = [256,256]
 DIRECT = [256,256]
@@ -77,8 +77,8 @@ def tile_picked_treeup_gelu_e_kernel(tc, xT, w1, w2_words, w2_scales, share, off
         pairs = [keep.tile([P, 2 * T], BF16, name="pairs%d" % u, align_bytes=64) for u in range(2)]
 
         def cast(engine, u, first, a, b):
-            dst = pairs[u][:, 2 * a : 2 * b].rearrange("p (s e) -> p s e", e=2)
-            src = raw[u, first][:, :, a - first : b - first].rearrange("p e s -> p s e")
+            dst = pairs[u][:, 2 * a : 2 * b].rearrange("p (c i e) -> p c e i", i=4, e=2)
+            src = raw[u, first][:, :, a - first : b - first].rearrange("p e (c i) -> p c e i", i=4)
             if engine == "v":
                 nc.vector.tensor_copy(out=dst, in_=src)
             else:
@@ -96,10 +96,12 @@ def tile_picked_treeup_gelu_e_kernel(tc, xT, w1, w2_words, w2_scales, share, off
         cast("s", 0, 1536, 1888, 2048)
         for a, b in spans(PICK):
             pick(0, a, b)
-        cast("s", 1, 0, 0, 1024)
-        cast("v", 1, 1024, 1024, 1536)
-        cast("v", 1, 1536, 1536, 1888)
-        cast("s", 1, 1536, 1888, 2048)
+        cast("s", 1, 0, 0, 768)
+        cast("s", 1, 768, 768, 1216)
+        cast("v", 1, 768, 1216, 1536)
+        cast("v", 1, 1536, 1536, 1792)
+        cast("v", 1, 1792, 1792, 1968)
+        cast("s", 1, 1792, 1968, 2048)
 
         wg = keep.tile([P, 4 * H], BF16, name="wg", align_bytes=64)
         for hh in range(2):
@@ -109,7 +111,7 @@ def tile_picked_treeup_gelu_e_kernel(tc, xT, w1, w2_words, w2_scales, share, off
         picks = spans(PICK)
         for a, b in picks:
             pick(1, a, b)
-        E = 512
+        E = 256
         xs = keep.tile([P, S], U8, name="xs", align_bytes=64)
         xq_early = keep.tile([P, E], U32, name="xq_early", align_bytes=64)
         xq_late = keep.tile([P, S - E], U32, name="xq_late", tag="wraw1", align_bytes=64)
@@ -119,35 +121,32 @@ def tile_picked_treeup_gelu_e_kernel(tc, xT, w1, w2_words, w2_scales, share, off
         def xq(a, b):
             return (xq_early[:, a:b] if b <= E else xq_late[:, a - E : b - E]).bitcast(FP8X4)
 
-        def quant_x(a):
-            nc.vector.quantize_mx(out=xq(a, a + 256), scales=xs[:, a : a + 256], in_=xg[a // 512 * 512][:, 4 * (a % 512) : 4 * (a % 512) + 1024])
+        def quant_x(a, b):
+            nc.vector.quantize_mx(out=xq(a, b), scales=xs[:, a:b], in_=xg[a // 512 * 512][:, 4 * (a % 512) : 4 * (a % 512) + 4 * (b - a)])
 
-        for a in range(0, E, 256):
-            quant_x(a)
+        steps = spans([256, 256, 256, 128, 128])
+        quant_x(0, E)
         nc.vector.quantize_mx(out=wq_first[:].bitcast(FP8X4), scales=ws[:, 0:P], in_=wg[:, 0:512])
-        for a in range(E, S, 256):
-            quant_x(a)
+        for a, b in steps[1:]:
+            quant_x(a, b)
         wq_rest = keep.tile([P, 3 * P], U32, name="wq_rest", align_bytes=64)
         nc.vector.quantize_mx(out=wq_rest[:, 0:P].bitcast(FP8X4), scales=ws[:, P : 2 * P], in_=wg[:, 512:1024])
         nc.vector.quantize_mx(out=wq_rest[:, P : 3 * P].bitcast(FP8X4), scales=ws[:, 2 * P : 4 * P], in_=wg[:, 1024:2048])
 
         h = [keep.tile([P, S], F32, name="h%d" % t, align_bytes=64) for t in range(4)]
         d0 = sum(PE_CH)
-        turns = keep.tile([P, 1792], F32, name="turns", align_bytes=64)
-        hc = turns[:, 0:768].rearrange("p (t s) -> p t s", t=4)[:, :, 0:P]
-        gd = turns[:, 0:1024].rearrange("p (t s) -> p t s", t=4)
-        zg_ab = turns[:, 768:1792].bitcast(BF16)
+        hc = keep.tile([P, 4, P], F32, name="hc")
         hd = keep.tile([P, 4, 384], F32, name="hd")
         for t in range(4):
             wq = (wq_first[:] if t == 0 else wq_rest[:, P * (t - 1) : P * t]).bitcast(FP8X4)
             if t == 0:
-                for (a, b), i in zip(spans([512, 256, 256]), (0, 6, 7)):
+                for (a, b), i in zip(steps, (0, 1, 6, 7, 0)):
                     acc = bank(i)[:, 0 : b - a]
                     nc.tensor.matmul_mx(out=acc, lhsT=wq, lhsT_scale=ws[:, 0:P], rhs=xq(a, b), rhs_scale=xs[:, a:b], start=True, stop=True)
                     nc.scalar.activation(out=h[0][:, a:b], in_=acc, func=GELU)
             else:
                 accs = [bank(2 * t), bank(2 * t + 1)]
-                for a, b in spans([512, 512]):
+                for a, b in spans([256, 256, 512]):
                     nc.tensor.matmul_mx(out=accs[a // 512][:, a % 512 : a % 512 + b - a], lhsT=wq, lhsT_scale=ws[:, P * t : P * t + P],
                                         rhs=xq(a, b), rhs_scale=xs[:, a:b], start=True, stop=True)
                     if b % 512 == 0:
@@ -195,25 +194,26 @@ def tile_picked_treeup_gelu_e_kernel(tc, xT, w1, w2_words, w2_scales, share, off
         for t in range(3):
             follow(g[:, t, :], t, 0, 768)
             turn(sums, t, g[:, t, :], 0)
-        for a in (0, 256, 512):
+        for a in (0, 512, 256):
             follow(g[:, 3, a : a + 256], 3, a, a + 256)
             if a < 512:
                 turn(sums[a // P : a // P + 2], 3, g[:, 3, a : a + 256], a)
         zg_c = keep.tile([P, 1024], BF16, name="zg_c", align_bytes=64)
-        for a, hh in ((0, hc), (P, hd[:, :, 0:P])):
+        for a, hh in ((0, hc[:]), (P, hd[:, :, 0:P])):
             nc.vector.tensor_tensor(out=zg_c[:, 4 * a : 4 * a + 512].rearrange("p (c i t) -> p c t i", i=4, t=4),
                                     in0=g[:, :, 512 + a : 512 + a + P].rearrange("p t (c i) -> p c t i", i=4),
                                     in1=hh.rearrange("p t (c i) -> p c t i", i=4), op=ADD)
         finish(zg_c[:], 512, 768, False, [6, 7], "ss")
+        zg_ab = keep.tile([P, 2048], BF16, name="zg_ab", align_bytes=64)
         for a, name in ((0, "a"), (256, "b")):
             back = bank(4 + a // 256)
             round_and_turn_back(sums[a // P : a // P + 2], [back[:, 0:256], back[:, 256:512]], name)
             weave(zg_ab[:, 4 * a : 4 * a + 1024], back[:], 2)
-        for t in range(3):
+        gd = keep.tile([P, 4, 256], F32, name="gd", tag="hc")
+        for t in range(4):
             follow(gd[:, t, :], t, 768, 1024)
-        finish(zg_ab, 0, 512, False, [0, 1], "ss")
-        follow(gd[:, 3, :], 3, 768, 1024)
-        zg_d = keep.tile([P, 1024], BF16, name="zg_d", align_bytes=64)
+        finish(zg_ab[:], 0, 512, False, [0, 1], "ss")
+        zg_d = keep.tile([P, 1024], BF16, name="zg_d", tag="zg_ab", align_bytes=64)
         for a in (0, 128):
             nc.vector.tensor_tensor(out=zg_d[:, 4 * a : 4 * a + 512].rearrange("p (c i t) -> p c t i", i=4, t=4),
                                     in0=gd[:, :, a : a + P].rearrange("p t (c i) -> p c t i", i=4),

@@ -74,6 +74,17 @@ def tile_picked_treeup_gelu_e_kernel(tc, xT, w1, w2_words, w2_scales, share, off
         for q in range(4):
             nc.sync.dma_start(w2s[32 * q : 32 * q + 4, :].bitcast(I32), w2_scales[0, 4 * q : 4 * q + 4, :].bitcast(I32))
 
+        zeros = keep.tile([P, 2048], BF16, name="zeros", align_bytes=64)
+        nc.vector.memset(zeros[:].bitcast(I32), 0)
+        zq0 = keep.tile([P, 512], U32, name="zeros_q", align_bytes=64)
+        zs0 = keep.tile([P, 512], U8, name="zeros_s", align_bytes=64)
+        nc.vector.quantize_mx(out=zq0[:].bitcast(FP8X4), scales=zs0[:], in_=zeros[:])
+        spare = bank(5)
+        nc.tensor.transpose(spare[:, 0:P], wraw[0][:, 0, 0:P], ident[:])
+        for i in range(3):
+            nc.tensor.matmul_mx(out=spare[:], lhsT=zq0[:, 0:P].bitcast(FP8X4), lhsT_scale=zs0[:, 0:P], rhs=zq0[:].bitcast(FP8X4), rhs_scale=zs0[:],
+                                start=True, stop=True)
+
         pairs = [keep.tile([P, 2 * T], BF16, name="pairs%d" % u, align_bytes=64) for u in range(2)]
 
         def cast(engine, u, first, a, b):

@@ -22,8 +22,6 @@ P = 128
 X0 = [1024,512,512]
 X1 = [768,768,256,256]
 PICK = [512,512]
-PE_CH = [256,256]
-DIRECT = [256,256]
 
 
 def spans(widths, start=0):
@@ -79,7 +77,7 @@ def tile_picked_treeup_gelu_e_kernel(tc, xT, w1, w2_words, w2_scales, share, off
         zq0 = keep.tile([P, 512], U32, name="zeros_q", align_bytes=64)
         zs0 = keep.tile([P, 512], U8, name="zeros_s", align_bytes=64)
         nc.vector.quantize_mx(out=zq0[:].bitcast(FP8X4), scales=zs0[:], in_=zeros[:])
-        spare = bank(5)
+        spare = bank(0)
         nc.tensor.transpose(spare[:, 0:P], wraw[0][:, 0, 0:P], ident[:])
         for i in range(3):
             nc.tensor.matmul_mx(out=spare[:], lhsT=zq0[:, 0:P].bitcast(FP8X4), lhsT_scale=zs0[:, 0:P], rhs=zq0[:].bitcast(FP8X4), rhs_scale=zs0[:],
@@ -145,89 +143,125 @@ def tile_picked_treeup_gelu_e_kernel(tc, xT, w1, w2_words, w2_scales, share, off
         nc.vector.quantize_mx(out=wq_rest[:, P : 3 * P].bitcast(FP8X4), scales=ws[:, 2 * P : 4 * P], in_=wg[:, 1024:2048])
 
         h = [keep.tile([P, S], F32, name="h%d" % t, align_bytes=64) for t in range(4)]
-        d0 = sum(PE_CH)
-        hc = keep.tile([P, 4, P], F32, name="hc")
-        hd = keep.tile([P, 4, 384], F32, name="hd")
+        hd = keep.tile([P, 4, 256], F32, name="hd")
         for t in range(4):
             wq = (wq_first[:] if t == 0 else wq_rest[:, P * (t - 1) : P * t]).bitcast(FP8X4)
             if t == 0:
-                for (a, b), i in zip(steps, (0, 1, 6, 7, 0)):
+                for (a, b), i in zip(steps, (3, 4, 5, 6, 7)):
                     acc = bank(i)[:, 0 : b - a]
                     nc.tensor.matmul_mx(out=acc, lhsT=wq, lhsT_scale=ws[:, 0:P], rhs=xq(a, b), rhs_scale=xs[:, a:b], start=True, stop=True)
                     nc.scalar.activation(out=h[0][:, a:b], in_=acc, func=GELU)
             else:
-                accs = [bank(2 * t), bank(2 * t + 1)]
+                accs = [bank(i) for i in ((3, 4), (6, 7), (5, 6))[t - 1]]
                 for a, b in spans([256, 256, 512]):
                     nc.tensor.matmul_mx(out=accs[a // 512][:, a % 512 : a % 512 + b - a], lhsT=wq, lhsT_scale=ws[:, P * t : P * t + P],
                                         rhs=xq(a, b), rhs_scale=xs[:, a:b], start=True, stop=True)
                     if b % 512 == 0:
                         nc.scalar.activation(out=h[t][:, b - 512 : b], in_=accs[a // 512][:], func=GELU)
-            nc.sync.dma_start(hc[:, t, :], h[t][:, 512:640])
-            nc.sync.dma_start(hd[:, t, :], h[t][:, 640:S])
+            nc.sync.dma_start(hd[:, t, :], h[t][:, 768:S])
 
         def follow(dst, t, a, b):
             nc.vector.tensor_tensor(out=dst, in0=h[t][:].indirect(par_t[:, a // 16 : b // 16]), in1=share_t[:, a:b], op=MULT)
 
-        def finish(zg, a, b, last, obanks, engines, slot=None):
-            n = b - a
-            zq = keep.tile([P, n], U32, name="zq%d" % a, tag=slot or "zq%d" % a, align_bytes=64)
-            zs = keep.tile([P, n], U8, name="zs%d" % a, align_bytes=64)
-            nc.vector.quantize_mx(out=zq[:].bitcast(FP8X4), scales=zs[:], in_=zg)
+        def turn(bk, e, src, first=False, last=False):
+            for c in range(2):
+                nc.tensor.matmul(out=bk[:, 256 * c + P * e : 256 * c + P * e + P], lhsT=src[:, P * c : P * c + P], rhs=ident[:], is_transpose=True,
+                                 start=first and c == 0, stop=last and c == 1)
+
+        def round_sums(bk, name):
+            zt = keep.tile([P, 512], BF16, name=name, align_bytes=64)
+            nc.scalar.copy(out=zt[:].rearrange("s (c p e) -> s c p e", c=2, e=2), in_=bk[:].rearrange("s (c e p) -> s c p e", c=2, e=2))
+            return zt
+
+        def turn_back(back, u, zt):
+            for c in range(2):
+                nc.tensor.transpose(back[:, 256 * c + P * u : 256 * c + P * u + P], zt[:].bitcast(F32)[:, P * c : P * c + P], ident[:])
+
+        def weave(back, name):
+            zg = keep.tile([P, 1024], BF16, name=name, align_bytes=64)
+            nc.scalar.copy(out=zg[:].bitcast(F32).rearrange("p (c s u) -> p c s u", c=2, u=2), in_=back[:].rearrange("p (c u s) -> p c s u", c=2, u=2))
+            return zg
+
+        def add(zg, gg, hh):
+            nc.vector.tensor_tensor(out=zg.rearrange("p (c i t) -> p c t i", i=4, t=4), in0=gg.rearrange("p t (c i) -> p c t i", i=4),
+                                    in1=hh.rearrange("p t (c i) -> p c t i", i=4), op=ADD)
+
+        def quant_z(zg, n, name, slot=None, calls=1):
+            zq = keep.tile([P, n], U32, name="zq" + name, tag=slot or "zq" + name, align_bytes=64)
+            zs = keep.tile([P, n], U8, name="zs" + name, align_bytes=64)
+            for a, b in spans([n // calls] * calls):
+                nc.vector.quantize_mx(out=zq[:, a:b].bitcast(FP8X4), scales=zs[:, a:b], in_=zg[:, 4 * a : 4 * b])
+            return zq, zs
+
+        def second(acc, mb, zq, zs):
+            nc.tensor.matmul_mx(out=acc, lhsT=w2w[:, 256 * mb : 256 * mb + 256].bitcast(FP4X4), lhsT_scale=w2s[:, P * mb : P * mb + P],
+                                rhs=zq[:].bitcast(FP8X4), rhs_scale=zs[:], start=True, stop=True)
+
+        out2 = out.rearrange("(mb p) s -> p mb s", mb=2)
+
+        def finish_one_bank(z, a, n, i):
+            acc = bank(i)
             for mb in range(2):
-                acc = bank(obanks[mb])
-                nc.tensor.matmul_mx(out=acc[:, 0:n], lhsT=w2w[:, 256 * mb : 256 * mb + 256].bitcast(FP4X4), lhsT_scale=w2s[:, P * mb : P * mb + P],
-                                    rhs=zq[:].bitcast(FP8X4), rhs_scale=zs[:], start=True, stop=True)
+                second(acc[:, n * mb : n * mb + n], mb, *z)
+            res = keep.tile([P, 2, n], F32, name="res%d" % a)
+            nc.scalar.copy(out=res[:].rearrange("p mb s -> p (mb s)"), in_=acc[:, 0 : 2 * n])
+            nc.sync.dma_start(out2[:, :, a : a + n], res[:])
+
+        def finish_two_banks(z, a, n, banks, last):
+            for mb in range(2):
+                acc = bank(banks[mb])
+                second(acc[:, 0:n], mb, *z)
                 res = keep.tile([P, n], F32, name="res%d_%d" % (a, mb))
-                if engines[mb] == "v":
+                if mb == 1:
                     nc.vector.tensor_copy(out=res[:], in_=acc[:, 0:n])
                 else:
                     nc.scalar.copy(out=res[:], in_=acc[:, 0:n])
-                (nc.scalar if last and engines[mb] == "s" else nc.sync).dma_start(out[P * mb : P * mb + P, a:b], res[:])
+                (nc.scalar if last and mb == 0 else nc.sync).dma_start(out[P * mb : P * mb + P, a : a + n], res[:])
 
-        def turn(banks, t, g, a):
-            for c, bk in enumerate(banks):
-                nc.tensor.matmul(out=bk[:, P * t : P * t + P], lhsT=h[t][:, a + P * c : a + P * c + P], rhs=ident[:], is_transpose=True, start=True, stop=False)
-            for c, bk in enumerate(banks):
-                nc.tensor.matmul(out=bk[:, P * t : P * t + P], lhsT=g[:, P * c : P * c + P], rhs=ident[:], is_transpose=True, start=False, stop=True)
-
-        def round_and_turn_back(banks, backs, name):
-            for c, bk in enumerate(banks):
-                zt = keep.tile([P, 512], BF16, name="zt%s%d" % (name, c), align_bytes=64)
-                nc.scalar.copy(out=zt[:].rearrange("s (u p e) -> s u p e", u=2, e=2), in_=bk[:].rearrange("s (u e p) -> s u p e", u=2, e=2))
-                for u in range(2):
-                    nc.tensor.transpose(backs[c][:, P * u : P * u + P], zt[:].bitcast(F32)[:, P * u : P * u + P], ident[:])
-
-        def weave(dst, back, blocks):
-            nc.scalar.copy(out=dst.bitcast(F32).rearrange("p (c s u) -> p c s u", c=blocks, u=2), in_=back.rearrange("p (c u s) -> p c s u", c=blocks, u=2))
-
-        sums = [bank(0), bank(1), bank(2), bank(3)]
+        sums = [[bank(0), bank(1), bank(2)], [bank(3), bank(4), bank(7)]]
         g = keep.tile([P, 4, 768], F32, name="g")
-        for t in range(3):
-            follow(g[:, t, :], t, 0, 768)
-            turn(sums, t, g[:, t, :], 0)
-        for a in (0, 512, 256):
-            follow(g[:, 3, a : a + 256], 3, a, a + 256)
-            if a < 512:
-                turn(sums[a // P : a // P + 2], 3, g[:, 3, a : a + 256], a)
-        zg_c = keep.tile([P, 1024], BF16, name="zg_c", align_bytes=64)
-        for a, hh in ((0, hc[:]), (P, hd[:, :, 0:P])):
-            nc.vector.tensor_tensor(out=zg_c[:, 4 * a : 4 * a + 512].rearrange("p (c i t) -> p c t i", i=4, t=4),
-                                    in0=g[:, :, 512 + a : 512 + a + P].rearrange("p t (c i) -> p c t i", i=4),
-                                    in1=hh.rearrange("p t (c i) -> p c t i", i=4), op=ADD)
-        finish(zg_c[:], 512, 768, False, [6, 7], "ss")
-        zg_ab = keep.tile([P, 2048], BF16, name="zg_ab", align_bytes=64)
-        for a, name in ((0, "a"), (256, "b")):
-            back = bank(4 + a // 256)
-            round_and_turn_back(sums[a // P : a // P + 2], [back[:, 0:256], back[:, 256:512]], name)
-            weave(zg_ab[:, 4 * a : 4 * a + 1024], back[:], 2)
-        gd = keep.tile([P, 4, 256], F32, name="gd", tag="hc")
+
+        def turn_all(src, t, **flag):
+            for q in range(3):
+                turn(sums[t // 2][q], t % 2, src[:, 256 * q : 256 * q + 256], **flag)
+
+        turn_all(h[0], 0, first=True)
+        turn_all(h[1], 1)
+        follow(g[:, 0, :], 0, 0, 768)
+        turn_all(g[:, 0, :], 0)
+        turn_all(h[2], 2, first=True)
+        turn_all(h[3], 3)
+        follow(g[:, 1, :], 1, 0, 768)
+        turn_all(g[:, 1, :], 1, last=True)
+        zt = [round_sums(sums[0][q], "zt0%d" % q) for q in range(3)]
+        backs = [bank(5), bank(6), bank(0)]
+        turn_back(backs[0], 0, zt[0])
+        follow(g[:, 2, :], 2, 0, 768)
+        turn_all(g[:, 2, :], 2)
+        for q in range(3):
+            follow(g[:, 3, 256 * q : 256 * q + 256], 3, 256 * q, 256 * q + 256)
+            turn(sums[1][q], 1, g[:, 3, 256 * q : 256 * q + 256], last=True)
+            if q < 2:
+                turn_back(backs[q + 1], 0, zt[q + 1])
+        zg = []
+        for q in range(3):
+            turn_back(backs[q], 1, round_sums(sums[1][q], "zt1%d" % q))
+            if q > 0:
+                zg.append(weave(backs[q - 1], "zg%d" % (q - 1)))
+        zg.append(weave(backs[2], "zg2"))
+        gd = keep.tile([P, 4, 256], F32, name="gd", tag="zt00", align_bytes=64)
         for t in range(4):
-            follow(gd[:, t, :], t, 768, 1024)
-        finish(zg_ab[:], 0, 512, False, [0, 1], "ss")
-        zg_d = keep.tile([P, 1024], BF16, name="zg_d", tag="zg_ab", align_bytes=64)
-        for a in (0, 128):
-            nc.vector.tensor_tensor(out=zg_d[:, 4 * a : 4 * a + 512].rearrange("p (c i t) -> p c t i", i=4, t=4),
-                                    in0=gd[:, :, a : a + P].rearrange("p t (c i) -> p c t i", i=4),
-                                    in1=hd[:, :, P + a : 2 * P + a].rearrange("p t (c i) -> p c t i", i=4), op=ADD)
-        finish(zg_d[:, 0:512], 768, 896, False, [2, 3], "ss")
-        finish(zg_d[:, 512:1024], 896, 1024, True, [4, 5], "sv")
+            follow(gd[:, t, :], t, 768, S)
+        zq_d = keep.tile([P, 256], U32, name="zq_d", align_bytes=64)
+        zs_d = keep.tile([P, 256], U8, name="zs_d", align_bytes=64)
+        zg_d = []
+        for q in range(2):
+            finish_one_bank(quant_z(zg[q], 256, "%d" % q), 256 * q, 256, 1 + q)
+        for q in range(2):
+            zg_d.append(keep.tile([P, 512], BF16, name="zg_d%d" % q, tag="zg%d" % q, align_bytes=64))
+            add(zg_d[q][:], gd[:, :, P * q : P * q + P], hd[:, :, P * q : P * q + P])
+            if q == 0:
+                finish_one_bank(quant_z(zg[2], 256, "2"), 512, 256, 3)
+        for q in range(2):
+            nc.vector.quantize_mx(out=zq_d[:, P * q : P * q + P].bitcast(FP8X4), scales=zs_d[:, P * q : P * q + P], in_=zg_d[q][:])
+        finish_two_banks((zq_d, zs_d), 768, 256, (4, 7), True)

@@ -65,8 +65,10 @@ def tile_picked_treeup_gelu_e_kernel(tc, xT, w1, w2_words, w2_scales, share, off
             wraw.append(keep.tile([P, 4, 256], F32, name="wraw%d" % hh, align_bytes=64))
             nc.sync.dma_start(wraw[hh][:], w4[:, :, 256 * hh : 256 * hh + 256])
         nc.sync.dma_start(par_t[:], par)
-        share_t = keep.tile([P, S], F32, name="share_t")
-        nc.sync.dma_start(share_t[:], share)
+        share_t = []
+        for hh in range(2):
+            share_t.append(keep.tile([P, 512], F32, name="share%d" % hh, align_bytes=64))
+            nc.sync.dma_start(share_t[hh][:], share[:, 512 * hh : 512 * hh + 512])
         w2w = keep.tile([P, 2 * N], U8, name="w2w", align_bytes=64)
         nc.sync.dma_start(w2w[:], w2_words[0])
         for q in range(4):
@@ -77,7 +79,7 @@ def tile_picked_treeup_gelu_e_kernel(tc, xT, w1, w2_words, w2_scales, share, off
         zq0 = keep.tile([P, 512], U32, name="zeros_q", align_bytes=64)
         zs0 = keep.tile([P, 512], U8, name="zeros_s", align_bytes=64)
         nc.vector.quantize_mx(out=zq0[:].bitcast(FP8X4), scales=zs0[:], in_=zeros[:])
-        spare = bank(0)
+        spare = bank(7)
         nc.tensor.transpose(spare[:, 0:P], wraw[0][:, 0, 0:P], ident[:])
         for i in range(3):
             nc.tensor.matmul_mx(out=spare[:], lhsT=zq0[:, 0:P].bitcast(FP8X4), lhsT_scale=zs0[:, 0:P], rhs=zq0[:].bitcast(FP8X4), rhs_scale=zs0[:],
@@ -147,12 +149,12 @@ def tile_picked_treeup_gelu_e_kernel(tc, xT, w1, w2_words, w2_scales, share, off
         for t in range(4):
             wq = (wq_first[:] if t == 0 else wq_rest[:, P * (t - 1) : P * t]).bitcast(FP8X4)
             if t == 0:
-                for (a, b), i in zip(steps, (3, 4, 5, 6, 7)):
+                for (a, b), i in zip(steps, (0, 1, 2, 3, 4)):
                     acc = bank(i)[:, 0 : b - a]
                     nc.tensor.matmul_mx(out=acc, lhsT=wq, lhsT_scale=ws[:, 0:P], rhs=xq(a, b), rhs_scale=xs[:, a:b], start=True, stop=True)
                     nc.scalar.activation(out=h[0][:, a:b], in_=acc, func=GELU)
             else:
-                accs = [bank(i) for i in ((3, 4), (6, 7), (5, 6))[t - 1]]
+                accs = [bank(i) for i in ((5, 6), (7, 3), (4, 5))[t - 1]]
                 for a, b in spans([256, 256, 512]):
                     nc.tensor.matmul_mx(out=accs[a // 512][:, a % 512 : a % 512 + b - a], lhsT=wq, lhsT_scale=ws[:, P * t : P * t + P],
                                         rhs=xq(a, b), rhs_scale=xs[:, a:b], start=True, stop=True)
@@ -161,7 +163,7 @@ def tile_picked_treeup_gelu_e_kernel(tc, xT, w1, w2_words, w2_scales, share, off
             nc.sync.dma_start(hd[:, t, :], h[t][:, 768:S])
 
         def follow(dst, t, a, b):
-            nc.vector.tensor_tensor(out=dst, in0=h[t][:].indirect(par_t[:, a // 16 : b // 16]), in1=share_t[:, a:b], op=MULT)
+            nc.vector.tensor_tensor(out=dst, in0=h[t][:].indirect(par_t[:, a // 16 : b // 16]), in1=share_t[a // 512][:, a % 512 : a % 512 + b - a], op=MULT)
 
         def turn(bk, e, src, first=False, last=False):
             for c in range(2):
@@ -177,48 +179,40 @@ def tile_picked_treeup_gelu_e_kernel(tc, xT, w1, w2_words, w2_scales, share, off
             for c in range(2):
                 nc.tensor.transpose(back[:, 256 * c + P * u : 256 * c + P * u + P], zt[:].bitcast(F32)[:, P * c : P * c + P], ident[:])
 
-        def weave(back, name):
-            zg = keep.tile([P, 1024], BF16, name=name, align_bytes=64)
-            nc.scalar.copy(out=zg[:].bitcast(F32).rearrange("p (c s u) -> p c s u", c=2, u=2), in_=back[:].rearrange("p (c u s) -> p c s u", c=2, u=2))
+        def weave(back, blocks, name):
+            zg = keep.tile([P, 512 * blocks], BF16, name=name, align_bytes=64)
+            nc.scalar.copy(out=zg[:].bitcast(F32).rearrange("p (c s u) -> p c s u", c=blocks, u=2), in_=back.rearrange("p (c u s) -> p c s u", c=blocks, u=2))
             return zg
 
         def add(zg, gg, hh):
             nc.vector.tensor_tensor(out=zg.rearrange("p (c i t) -> p c t i", i=4, t=4), in0=gg.rearrange("p t (c i) -> p c t i", i=4),
                                     in1=hh.rearrange("p t (c i) -> p c t i", i=4), op=ADD)
 
-        def quant_z(zg, n, name, slot=None, calls=1):
+        def quant_z(parts, name, slot=None):
+            n = sum(part.shape[1] for part in parts) // 4
             zq = keep.tile([P, n], U32, name="zq" + name, tag=slot or "zq" + name, align_bytes=64)
             zs = keep.tile([P, n], U8, name="zs" + name, align_bytes=64)
-            for a, b in spans([n // calls] * calls):
-                nc.vector.quantize_mx(out=zq[:, a:b].bitcast(FP8X4), scales=zs[:, a:b], in_=zg[:, 4 * a : 4 * b])
+            for part, (a, b) in zip(parts, spans([part.shape[1] // 4 for part in parts])):
+                nc.vector.quantize_mx(out=zq[:, a:b].bitcast(FP8X4), scales=zs[:, a:b], in_=part)
             return zq, zs
 
         def second(acc, mb, zq, zs):
             nc.tensor.matmul_mx(out=acc, lhsT=w2w[:, 256 * mb : 256 * mb + 256].bitcast(FP4X4), lhsT_scale=w2s[:, P * mb : P * mb + P],
                                 rhs=zq[:].bitcast(FP8X4), rhs_scale=zs[:], start=True, stop=True)
 
-        out2 = out.rearrange("(mb p) s -> p mb s", mb=2)
-
-        def finish_one_bank(z, a, n, i):
-            acc = bank(i)
+        def product_two_banks(z, n, banks):
+            accs = [bank(i)[:, 0:n] for i in banks]
             for mb in range(2):
-                second(acc[:, n * mb : n * mb + n], mb, *z)
-            res = keep.tile([P, 2, n], F32, name="res%d" % a)
-            nc.scalar.copy(out=res[:].rearrange("p mb s -> p (mb s)"), in_=acc[:, 0 : 2 * n])
-            nc.sync.dma_start(out2[:, :, a : a + n], res[:])
+                second(accs[mb], mb, *z)
+            return accs
 
-        def finish_two_banks(z, a, n, banks, last):
-            for mb in range(2):
-                acc = bank(banks[mb])
-                second(acc[:, 0:n], mb, *z)
-                res = keep.tile([P, n], F32, name="res%d_%d" % (a, mb))
-                if mb == 1:
-                    nc.vector.tensor_copy(out=res[:], in_=acc[:, 0:n])
-                else:
-                    nc.scalar.copy(out=res[:], in_=acc[:, 0:n])
-                (nc.scalar if last and mb == 0 else nc.sync).dma_start(out[P * mb : P * mb + P, a : a + n], res[:])
+        def finish_by_scalar(z, a, banks):
+            for mb, acc in enumerate(product_two_banks(z, 256, banks)):
+                res = keep.tile([P, 256], F32, name="res%d_%d" % (a, mb))
+                nc.scalar.copy(out=res[:], in_=acc)
+                nc.sync.dma_start(out[P * mb : P * mb + P, a : a + 256], res[:])
 
-        sums = [[bank(0), bank(1), bank(2)], [bank(3), bank(4), bank(7)]]
+        sums = [[bank(0), bank(1), bank(2)], [bank(6), bank(7), bank(3)]]
         g = keep.tile([P, 4, 768], F32, name="g")
 
         def turn_all(src, t, **flag):
@@ -227,41 +221,47 @@ def tile_picked_treeup_gelu_e_kernel(tc, xT, w1, w2_words, w2_scales, share, off
 
         turn_all(h[0], 0, first=True)
         turn_all(h[1], 1)
-        follow(g[:, 0, :], 0, 0, 768)
+        follow(g[:, 0, 0:512], 0, 0, 512)
+        follow(g[:, 0, 512:768], 0, 512, 768)
         turn_all(g[:, 0, :], 0)
         turn_all(h[2], 2, first=True)
         turn_all(h[3], 3)
-        follow(g[:, 1, :], 1, 0, 768)
+        follow(g[:, 1, 0:512], 1, 0, 512)
+        follow(g[:, 1, 512:768], 1, 512, 768)
         turn_all(g[:, 1, :], 1, last=True)
         zt = [round_sums(sums[0][q], "zt0%d" % q) for q in range(3)]
-        backs = [bank(5), bank(6), bank(0)]
+        backs = [bank(4), bank(5), bank(0)]
         turn_back(backs[0], 0, zt[0])
-        follow(g[:, 2, :], 2, 0, 768)
+        follow(g[:, 2, 0:512], 2, 0, 512)
+        follow(g[:, 2, 512:768], 2, 512, 768)
         turn_all(g[:, 2, :], 2)
         for q in range(3):
             follow(g[:, 3, 256 * q : 256 * q + 256], 3, 256 * q, 256 * q + 256)
             turn(sums[1][q], 1, g[:, 3, 256 * q : 256 * q + 256], last=True)
             if q < 2:
                 turn_back(backs[q + 1], 0, zt[q + 1])
-        zg = []
         for q in range(3):
             turn_back(backs[q], 1, round_sums(sums[1][q], "zt1%d" % q))
-            if q > 0:
-                zg.append(weave(backs[q - 1], "zg%d" % (q - 1)))
-        zg.append(weave(backs[2], "zg2"))
-        gd = keep.tile([P, 4, 256], F32, name="gd", tag="zt00", align_bytes=64)
+        zg0 = [weave(backs[0][:, 256 * c : 256 * c + 256], 1, "zg0%d" % c) for c in range(2)]
+        zg1 = weave(backs[1][:], 2, "zg1")
+        zg2 = weave(backs[2][:], 2, "zg2")
+        gd = keep.tile([P, 4, 256], F32, name="gd", tag="share0", align_bytes=64)
         for t in range(4):
             follow(gd[:, t, :], t, 768, S)
-        zq_d = keep.tile([P, 256], U32, name="zq_d", align_bytes=64)
-        zs_d = keep.tile([P, 256], U8, name="zs_d", align_bytes=64)
+        finish_by_scalar(quant_z([part[:] for part in zg0], "0"), 0, (1, 2))
+        finish_by_scalar(quant_z([zg1[:]], "1"), 256, (3, 4))
         zg_d = []
         for q in range(2):
-            finish_one_bank(quant_z(zg[q], 256, "%d" % q), 256 * q, 256, 1 + q)
-        for q in range(2):
-            zg_d.append(keep.tile([P, 512], BF16, name="zg_d%d" % q, tag="zg%d" % q, align_bytes=64))
+            zg_d.append(keep.tile([P, 512], BF16, name="zg_d%d" % q, tag=("zg00", "zg1")[q], align_bytes=64))
             add(zg_d[q][:], gd[:, :, P * q : P * q + P], hd[:, :, P * q : P * q + P])
             if q == 0:
-                finish_one_bank(quant_z(zg[2], 256, "2"), 512, 256, 3)
-        for q in range(2):
-            nc.vector.quantize_mx(out=zq_d[:, P * q : P * q + P].bitcast(FP8X4), scales=zs_d[:, P * q : P * q + P], in_=zg_d[q][:])
-        finish_two_banks((zq_d, zs_d), 768, 256, (4, 7), True)
+                last = [(product_two_banks(quant_z([zg2[:]], "2"), 256, (6, 7)), 0, 256)]
+        for q, banks in enumerate(((5, 0), (1, 2))):
+            last.append((product_two_banks(quant_z([zg_d[q][:]], "d%d" % q, slot=("zg2", None)[q]), P, banks), 256 + P * q, 384 + P * q))
+        res = [keep.tile([P, 512], F32, name="res_last%d" % mb, tag=("res_last0", "zg1")[mb], align_bytes=64) for mb in range(2)]
+        for accs, a, b in last:
+            nc.scalar.copy(out=res[0][:, a:b], in_=accs[0])
+            nc.vector.tensor_copy(out=res[1][:, a:b], in_=accs[1])
+            if b % 256 == 0:
+                (nc.scalar if b == 512 else nc.sync).dma_start(out[0:P, 256 + b : 512 + b], res[0][:, b - 256 : b])
+                nc.sync.dma_start(out[P : 2 * P, 256 + b : 512 + b], res[1][:, b - 256 : b])

@@ -21,7 +21,6 @@ ADD = mybir.AluOpType.add
 P = 128
 X0 = [1024,512,512]
 X1 = [768,768,256,256]
-PICK = [512,512]
 
 
 def spans(widths, start=0):
@@ -61,9 +60,9 @@ def tile_picked_treeup_gelu_e_kernel(tc, xT, w1, w2_words, w2_scales, share, off
                     nc.sync.dma_start(offs_t[:], offs)
         w4 = w1.rearrange("(p j) c -> p j c", j=4)
         wraw = []
-        for hh in range(2):
-            wraw.append(keep.tile([P, 4, 256], F32, name="wraw%d" % hh, align_bytes=64))
-            nc.sync.dma_start(wraw[hh][:], w4[:, :, 256 * hh : 256 * hh + 256])
+        for hh in range(4):
+            wraw.append(keep.tile([P, 4, P], F32, name="wraw%d" % hh, align_bytes=64))
+            nc.sync.dma_start(wraw[hh][:], w4[:, :, P * hh : P * hh + P])
         nc.sync.dma_start(par_t[:], par)
         share_t = []
         for hh in range(2):
@@ -80,7 +79,7 @@ def tile_picked_treeup_gelu_e_kernel(tc, xT, w1, w2_words, w2_scales, share, off
         zs0 = keep.tile([P, 512], U8, name="zeros_s", align_bytes=64)
         nc.vector.quantize_mx(out=zq0[:].bitcast(FP8X4), scales=zs0[:], in_=zeros[:])
         spare = bank(7)
-        nc.tensor.transpose(spare[:, 0:P], wraw[0][:, 0, 0:P], ident[:])
+        nc.tensor.transpose(spare[:, 0:P], wraw[1][:, 0, 0:P], ident[:])
         for i in range(3):
             nc.tensor.matmul_mx(out=spare[:], lhsT=zq0[:, 0:P].bitcast(FP8X4), lhsT_scale=zs0[:, 0:P], rhs=zq0[:].bitcast(FP8X4), rhs_scale=zs0[:],
                                 start=True, stop=True)
@@ -95,18 +94,21 @@ def tile_picked_treeup_gelu_e_kernel(tc, xT, w1, w2_words, w2_scales, share, off
             else:
                 nc.scalar.copy(out=dst, in_=src)
 
-        xg = {a: keep.tile([P, 4 * (b - a)], BF16, name="xg%d" % a, align_bytes=64) for a, b in spans(PICK)}
+        rows = keep.tile([P, 2, 512], U32, name="rows", align_bytes=64)
+        xg_b = keep.tile([P, 2048], BF16, name="xg_b", align_bytes=64)
 
-        def pick(u, a, b):
-            dst = xg[a][:].bitcast(U32).rearrange("p (s u) -> p s u", u=2)[:, :, u]
-            nc.vector.tensor_copy(out=dst, in_=pairs[u][:].bitcast(U32).indirect(offs_t[:, a // 16 : b // 16]))
+        def pick(u):
+            window = pairs[u][:].bitcast(U32)
+            nc.vector.tensor_copy(out=rows[:, u, :], in_=window.indirect(offs_t[:, 0:32]))
+            for a in (0, 256):
+                dst = xg_b[:].bitcast(U32).rearrange("p (s u) -> p s u", u=2)[:, a : a + 256, u]
+                nc.vector.tensor_copy(out=dst, in_=window.indirect(offs_t[:, 32 + a // 16 : 48 + a // 16]))
 
         cast("v", 0, 0, 0, 1024)
         cast("s", 0, 1024, 1024, 1536)
         cast("v", 0, 1536, 1536, 1888)
         cast("s", 0, 1536, 1888, 2048)
-        for a, b in spans(PICK):
-            pick(0, a, b)
+        pick(0)
         cast("s", 1, 0, 0, 768)
         cast("s", 1, 768, 768, 1216)
         cast("v", 1, 768, 1216, 1536)
@@ -115,32 +117,29 @@ def tile_picked_treeup_gelu_e_kernel(tc, xT, w1, w2_words, w2_scales, share, off
         cast("s", 1, 1792, 1968, 2048)
 
         wg = keep.tile([P, 4 * H], BF16, name="wg", align_bytes=64)
-        for hh in range(2):
-            dst = wg[:].rearrange("p (t m j) -> p m j t", t=4, j=4)[:, 64 * hh : 64 * hh + 64, :, :]
+        for hh in range(4):
+            dst = wg[:].rearrange("p (t m j) -> p m j t", t=4, j=4)[:, 32 * hh : 32 * hh + 32, :, :]
             nc.scalar.copy(out=dst, in_=wraw[hh][:].rearrange("p j (m t) -> p m j t", t=4))
 
-        picks = spans(PICK)
-        for a, b in picks:
-            pick(1, a, b)
-        E = 256
+        pick(1)
+        xg_a = keep.tile([P, 1024], U32, name="xg_a", tag="wraw2", align_bytes=64)
+        for a in (0, 256):
+            nc.scalar.copy(out=xg_a[:, 2 * a : 2 * a + 512].rearrange("p (c i u) -> p c u i", i=4, u=2),
+                           in_=rows[:, :, a : a + 256].rearrange("p u (c i) -> p c u i", i=4))
         xs = keep.tile([P, S], U8, name="xs", align_bytes=64)
-        xq_early = keep.tile([P, E], U32, name="xq_early", align_bytes=64)
-        xq_late = keep.tile([P, S - E], U32, name="xq_late", tag="wraw1", align_bytes=64)
+        xq_t = keep.tile([P, S], U32, name="xq_t", tag="wraw3", align_bytes=64)
         ws = keep.tile([P, H], U8, name="ws", align_bytes=64)
         wq_first = keep.tile([P, P], U32, name="wq_first", align_bytes=64)
 
         def xq(a, b):
-            return (xq_early[:, a:b] if b <= E else xq_late[:, a - E : b - E]).bitcast(FP8X4)
+            return xq_t[:, a:b].bitcast(FP8X4)
 
-        def quant_x(a, b):
-            nc.vector.quantize_mx(out=xq(a, b), scales=xs[:, a:b], in_=xg[a // 512 * 512][:, 4 * (a % 512) : 4 * (a % 512) + 4 * (b - a)])
-
-        steps = spans([256, 256, 256, 128, 128])
-        quant_x(0, E)
+        steps = [(512, 768), (768, S), (0, 256), (256, 384), (384, 512)]
         nc.vector.quantize_mx(out=wq_first[:].bitcast(FP8X4), scales=ws[:, 0:P], in_=wg[:, 0:512])
-        for a, b in steps[1:]:
-            quant_x(a, b)
-        wq_rest = keep.tile([P, 3 * P], U32, name="wq_rest", align_bytes=64)
+        for a, b in steps:
+            src = xg_a[:].bitcast(BF16)[:, 4 * a : 4 * b] if a < 512 else xg_b[:, 4 * a - 2048 : 4 * b - 2048]
+            nc.vector.quantize_mx(out=xq(a, b), scales=xs[:, a:b], in_=src)
+        wq_rest = keep.tile([P, 3 * P], U32, name="wq_rest", tag="wraw2", align_bytes=64)
         nc.vector.quantize_mx(out=wq_rest[:, 0:P].bitcast(FP8X4), scales=ws[:, P : 2 * P], in_=wg[:, 512:1024])
         nc.vector.quantize_mx(out=wq_rest[:, P : 3 * P].bitcast(FP8X4), scales=ws[:, 2 * P : 4 * P], in_=wg[:, 1024:2048])
 
@@ -155,7 +154,7 @@ def tile_picked_treeup_gelu_e_kernel(tc, xT, w1, w2_words, w2_scales, share, off
                     nc.scalar.activation(out=h[0][:, a:b], in_=acc, func=GELU)
             else:
                 accs = [bank(i) for i in ((5, 6), (7, 3), (4, 5))[t - 1]]
-                for a, b in spans([256, 256, 512]):
+                for a, b in spans([512, 512]):
                     nc.tensor.matmul_mx(out=accs[a // 512][:, a % 512 : a % 512 + b - a], lhsT=wq, lhsT_scale=ws[:, P * t : P * t + P],
                                         rhs=xq(a, b), rhs_scale=xs[:, a:b], start=True, stop=True)
                     if b % 512 == 0:
@@ -230,8 +229,7 @@ def tile_picked_treeup_gelu_e_kernel(tc, xT, w1, w2_words, w2_scales, share, off
         follow(g[:, 1, 512:768], 1, 512, 768)
         turn_all(g[:, 1, :], 1, last=True)
         zt = [round_sums(sums[0][q], "zt0%d" % q) for q in range(3)]
-        backs = [bank(4), bank(5), bank(0)]
-        turn_back(backs[0], 0, zt[0])
+        backs = [bank(4), bank(5)]
         follow(g[:, 2, 0:512], 2, 0, 512)
         follow(g[:, 2, 512:768], 2, 512, 768)
         turn_all(g[:, 2, :], 2)
@@ -239,8 +237,11 @@ def tile_picked_treeup_gelu_e_kernel(tc, xT, w1, w2_words, w2_scales, share, off
             follow(g[:, 3, 256 * q : 256 * q + 256], 3, 256 * q, 256 * q + 256)
             turn(sums[1][q], 1, g[:, 3, 256 * q : 256 * q + 256], last=True)
             if q < 2:
-                turn_back(backs[q + 1], 0, zt[q + 1])
-        for q in range(3):
+                turn_back(backs[q], 0, zt[q])
+        turn_back(backs[0], 1, round_sums(sums[1][0], "zt10"))
+        backs.append(bank(6))
+        turn_back(backs[2], 0, zt[2])
+        for q in (1, 2):
             turn_back(backs[q], 1, round_sums(sums[1][q], "zt1%d" % q))
         zg0 = [weave(backs[0][:, 256 * c : 256 * c + 256], 1, "zg0%d" % c) for c in range(2)]
         zg1 = weave(backs[1][:], 2, "zg1")
@@ -255,8 +256,8 @@ def tile_picked_treeup_gelu_e_kernel(tc, xT, w1, w2_words, w2_scales, share, off
             zg_d.append(keep.tile([P, 512], BF16, name="zg_d%d" % q, tag=("zg00", "zg1")[q], align_bytes=64))
             add(zg_d[q][:], gd[:, :, P * q : P * q + P], hd[:, :, P * q : P * q + P])
             if q == 0:
-                last = [(product_two_banks(quant_z([zg2[:]], "2"), 256, (6, 7)), 0, 256)]
-        for q, banks in enumerate(((5, 0), (1, 2))):
+                last = [(product_two_banks(quant_z([zg2[:]], "2"), 256, (0, 7)), 0, 256)]
+        for q, banks in enumerate(((5, 6), (1, 2))):
             last.append((product_two_banks(quant_z([zg_d[q][:]], "d%d" % q, slot=("zg2", None)[q]), P, banks), 256 + P * q, 384 + P * q))
         res = [keep.tile([P, 512], F32, name="res_last%d" % mb, tag=("res_last0", "zg1")[mb], align_bytes=64) for mb in range(2)]
         for accs, a, b in last:

@@ -73,17 +73,6 @@ def tile_picked_treeup_gelu_e_kernel(tc, xT, w1, w2_words, w2_scales, share, off
         for q in range(4):
             nc.sync.dma_start(w2s[32 * q : 32 * q + 4, :].bitcast(I32), w2_scales[0, 4 * q : 4 * q + 4, :].bitcast(I32))
 
-        zeros = keep.tile([P, 2048], BF16, name="zeros", align_bytes=64)
-        nc.vector.memset(zeros[:].bitcast(I32), 0)
-        zq0 = keep.tile([P, 512], U32, name="zeros_q", align_bytes=64)
-        zs0 = keep.tile([P, 512], U8, name="zeros_s", align_bytes=64)
-        nc.vector.quantize_mx(out=zq0[:].bitcast(FP8X4), scales=zs0[:], in_=zeros[:])
-        spare = bank(7)
-        nc.tensor.transpose(spare[:, 0:P], wraw[1][:, 0, 0:P], ident[:])
-        for i in range(3):
-            nc.tensor.matmul_mx(out=spare[:], lhsT=zq0[:, 0:P].bitcast(FP8X4), lhsT_scale=zs0[:, 0:P], rhs=zq0[:].bitcast(FP8X4), rhs_scale=zs0[:],
-                                start=True, stop=True)
-
         pairs = [keep.tile([P, 2 * T], BF16, name="pairs%d" % u, align_bytes=64) for u in range(2)]
 
         def cast(engine, u, first, a, b):
@@ -94,17 +83,22 @@ def tile_picked_treeup_gelu_e_kernel(tc, xT, w1, w2_words, w2_scales, share, off
             else:
                 nc.scalar.copy(out=dst, in_=src)
 
-        rows = keep.tile([P, 2, 512], U32, name="rows", align_bytes=64)
-        xg_b = keep.tile([P, 2048], BF16, name="xg_b", align_bytes=64)
+        rows = [keep.tile([P, 2, 256], U32, name="rows%d" % q, align_bytes=64) for q in range(4)]
 
         def pick(u):
             window = pairs[u][:].bitcast(U32)
-            nc.vector.tensor_copy(out=rows[:, u, :], in_=window.indirect(offs_t[:, 0:32]))
-            for a in (0, 256):
-                dst = xg_b[:].bitcast(U32).rearrange("p (s u) -> p s u", u=2)[:, a : a + 256, u]
-                nc.vector.tensor_copy(out=dst, in_=window.indirect(offs_t[:, 32 + a // 16 : 48 + a // 16]))
+            for q in range(4):
+                nc.vector.tensor_copy(out=rows[q][:, u, :], in_=window.indirect(offs_t[:, 16 * q : 16 * q + 16]))
 
         cast("v", 0, 0, 0, 1024)
+        warm_q = keep.tile([P, 512], U32, name="warm_q", align_bytes=64)
+        warm_s = keep.tile([P, 512], U8, name="warm_s", align_bytes=64)
+        nc.vector.quantize_mx(out=warm_q[:].bitcast(FP8X4), scales=warm_s[:], in_=pairs[0][:, 0:2048])
+        spare = bank(7)
+        nc.tensor.transpose(spare[:, 0:P], wraw[1][:, 0, 0:P], ident[:])
+        for i in range(3):
+            nc.tensor.matmul_mx(out=spare[:], lhsT=warm_q[:, 0:P].bitcast(FP8X4), lhsT_scale=warm_s[:, 0:P], rhs=warm_q[:].bitcast(FP8X4), rhs_scale=warm_s[:],
+                                start=True, stop=True)
         cast("s", 0, 1024, 1024, 1536)
         cast("v", 0, 1536, 1536, 1888)
         cast("s", 0, 1536, 1888, 2048)
@@ -122,10 +116,13 @@ def tile_picked_treeup_gelu_e_kernel(tc, xT, w1, w2_words, w2_scales, share, off
             nc.scalar.copy(out=dst, in_=wraw[hh][:].rearrange("p j (m t) -> p m j t", t=4))
 
         pick(1)
-        xg_a = keep.tile([P, 1024], U32, name="xg_a", tag="wraw2", align_bytes=64)
-        for a in (0, 256):
-            nc.scalar.copy(out=xg_a[:, 2 * a : 2 * a + 512].rearrange("p (c i u) -> p c u i", i=4, u=2),
-                           in_=rows[:, :, a : a + 256].rearrange("p u (c i) -> p c u i", i=4))
+        xg_a = keep.tile([P, 1024], U32, name="xg_a", align_bytes=64)
+        xg_b = keep.tile([P, 1024], U32, name="xg_b", tag="wraw2", align_bytes=64)
+        for q in range(2):
+            nc.gpsimd.tensor_copy(out=xg_a[:, 512 * q : 512 * q + 512].rearrange("p (s u) -> p s u", u=2), in_=rows[q][:].rearrange("p u s -> p s u"))
+        for q in range(2):
+            nc.scalar.copy(out=xg_b[:, 512 * q : 512 * q + 512].rearrange("p (c i u) -> p c u i", i=4, u=2),
+                           in_=rows[2 + q][:].rearrange("p u (c i) -> p c u i", i=4))
         xs = keep.tile([P, S], U8, name="xs", align_bytes=64)
         xq_t = keep.tile([P, S], U32, name="xq_t", tag="wraw3", align_bytes=64)
         ws = keep.tile([P, H], U8, name="ws", align_bytes=64)
@@ -134,10 +131,10 @@ def tile_picked_treeup_gelu_e_kernel(tc, xT, w1, w2_words, w2_scales, share, off
         def xq(a, b):
             return xq_t[:, a:b].bitcast(FP8X4)
 
-        steps = [(512, 768), (768, S), (0, 256), (256, 384), (384, 512)]
+        steps = [(0, 256), (256, 512), (512, 768), (768, 896), (896, S)]
         nc.vector.quantize_mx(out=wq_first[:].bitcast(FP8X4), scales=ws[:, 0:P], in_=wg[:, 0:512])
         for a, b in steps:
-            src = xg_a[:].bitcast(BF16)[:, 4 * a : 4 * b] if a < 512 else xg_b[:, 4 * a - 2048 : 4 * b - 2048]
+            src = xg_a[:].bitcast(BF16)[:, 4 * a : 4 * b] if a < 512 else xg_b[:].bitcast(BF16)[:, 4 * a - 2048 : 4 * b - 2048]
             nc.vector.quantize_mx(out=xq(a, b), scales=xs[:, a:b], in_=src)
         wq_rest = keep.tile([P, 3 * P], U32, name="wq_rest", tag="wraw2", align_bytes=64)
         nc.vector.quantize_mx(out=wq_rest[:, 0:P].bitcast(FP8X4), scales=ws[:, P : 2 * P], in_=wg[:, 512:1024])

@@ -35,6 +35,7 @@ def tile_picked_treeup_gelu_e_kernel(tc, xT, w1, w2_words, w2_scales, share, off
     nc = tc.nc
     with ExitStack() as ctx:
         keep = ctx.enter_context(tc.tile_pool(name="keep", bufs=1))
+        placed = ctx.enter_context(tc.tile_pool(name="placed", bufs=1))
         psum = ctx.enter_context(tc.psum_pool(name="psum", bufs=1))
 
         def bank(i):
@@ -61,7 +62,10 @@ def tile_picked_treeup_gelu_e_kernel(tc, xT, w1, w2_words, w2_scales, share, off
         w4 = w1.rearrange("(p j) c -> p j c", j=4)
         wraw = []
         for hh in range(4):
-            wraw.append(keep.tile([P, 4, P], F32, name="wraw%d" % hh, align_bytes=64))
+            if hh < 3:
+                wraw.append(keep.tile([P, 4, P], F32, name="wraw%d" % hh, align_bytes=64))
+            else:
+                wraw.append(placed.tile([P, 4, P], F32, name="wraw3", align_bytes=64, offset=1024))
             nc.sync.dma_start(wraw[hh][:], w4[:, :, P * hh : P * hh + P])
         nc.sync.dma_start(par_t[:], par)
         share_t = []
@@ -83,19 +87,21 @@ def tile_picked_treeup_gelu_e_kernel(tc, xT, w1, w2_words, w2_scales, share, off
             else:
                 nc.scalar.copy(out=dst, in_=src)
 
-        rows = [keep.tile([P, 2, 256], U32, name="rows%d" % q, align_bytes=64) for q in range(4)]
+        rows = [keep.tile([P, 2, 256], U32, name="rows%d" % q, align_bytes=64) for q in range(3)]
+        xg_d = keep.tile([P, 512], U32, name="xg_d", align_bytes=64)
 
         def pick(u):
             window = pairs[u][:].bitcast(U32)
-            for q in range(4):
+            for q in range(3):
                 nc.vector.tensor_copy(out=rows[q][:, u, :], in_=window.indirect(offs_t[:, 16 * q : 16 * q + 16]))
+            nc.vector.tensor_copy(out=xg_d[:].rearrange("p (s u) -> p s u", u=2)[:, :, u], in_=window.indirect(offs_t[:, 48:64]))
 
         cast("v", 0, 0, 0, 1024)
         warm_q = keep.tile([P, 512], U32, name="warm_q", align_bytes=64)
         warm_s = keep.tile([P, 512], U8, name="warm_s", align_bytes=64)
         nc.vector.quantize_mx(out=warm_q[:].bitcast(FP8X4), scales=warm_s[:], in_=pairs[0][:, 0:2048])
         spare = bank(7)
-        nc.tensor.transpose(spare[:, 0:P], wraw[1][:, 0, 0:P], ident[:])
+        nc.tensor.transpose(spare[:, 0:P], wraw[0][:, 0, 0:P], ident[:])
         for i in range(3):
             nc.tensor.matmul_mx(out=spare[:], lhsT=warm_q[:, 0:P].bitcast(FP8X4), lhsT_scale=warm_s[:, 0:P], rhs=warm_q[:].bitcast(FP8X4), rhs_scale=warm_s[:],
                                 start=True, stop=True)
@@ -113,30 +119,32 @@ def tile_picked_treeup_gelu_e_kernel(tc, xT, w1, w2_words, w2_scales, share, off
         wg = keep.tile([P, 4 * H], BF16, name="wg", align_bytes=64)
         for hh in range(4):
             dst = wg[:].rearrange("p (t m j) -> p m j t", t=4, j=4)[:, 32 * hh : 32 * hh + 32, :, :]
-            nc.scalar.copy(out=dst, in_=wraw[hh][:].rearrange("p j (m t) -> p m j t", t=4))
+            src = wraw[hh][:].rearrange("p j (m t) -> p m j t", t=4)
+            for a, b in spans([4] if hh < 3 else [2, 2]):
+                nc.scalar.copy(out=dst[:, :, :, a:b], in_=src[:, :, :, a:b])
 
         pick(1)
         xg_a = keep.tile([P, 1024], U32, name="xg_a", align_bytes=64)
-        xg_b = keep.tile([P, 1024], U32, name="xg_b", tag="wraw2", align_bytes=64)
+        xg_c = placed.tile([P, 512], U32, name="xg_c", align_bytes=64, offset=0)
         for q in range(2):
             nc.gpsimd.tensor_copy(out=xg_a[:, 512 * q : 512 * q + 512].rearrange("p (s u) -> p s u", u=2), in_=rows[q][:].rearrange("p u s -> p s u"))
-        for q in range(2):
-            nc.scalar.copy(out=xg_b[:, 512 * q : 512 * q + 512].rearrange("p (c i u) -> p c u i", i=4, u=2),
-                           in_=rows[2 + q][:].rearrange("p u (c i) -> p c u i", i=4))
+        nc.scalar.copy(out=xg_c[:].rearrange("p (c i u) -> p c u i", i=4, u=2), in_=rows[2][:].rearrange("p u (c i) -> p c u i", i=4))
         xs = keep.tile([P, S], U8, name="xs", align_bytes=64)
-        xq_t = keep.tile([P, S], U32, name="xq_t", tag="wraw3", align_bytes=64)
+        xq_first = keep.tile([P, 256], U32, name="xq_first", align_bytes=64)
+        xq_t = placed.tile([P, S - 256], U32, name="xq_t", align_bytes=64, offset=2048)
         ws = keep.tile([P, H], U8, name="ws", align_bytes=64)
         wq_first = keep.tile([P, P], U32, name="wq_first", align_bytes=64)
 
         def xq(a, b):
-            return xq_t[:, a:b].bitcast(FP8X4)
+            return (xq_first[:, a:b] if a < 256 else xq_t[:, a - 256 : b - 256]).bitcast(FP8X4)
 
-        steps = [(0, 256), (256, 512), (512, 768), (768, 896), (896, S)]
+        steps = [(0, 256), (256, 512), (768, S), (512, 640), (640, 768)]
         nc.vector.quantize_mx(out=wq_first[:].bitcast(FP8X4), scales=ws[:, 0:P], in_=wg[:, 0:512])
         for a, b in steps:
-            src = xg_a[:].bitcast(BF16)[:, 4 * a : 4 * b] if a < 512 else xg_b[:].bitcast(BF16)[:, 4 * a - 2048 : 4 * b - 2048]
+            part, first = (xg_a, 0) if a < 512 else (xg_c, 512) if a < 768 else (xg_d, 768)
+            src = part[:].bitcast(BF16)[:, 4 * (a - first) : 4 * (b - first)]
             nc.vector.quantize_mx(out=xq(a, b), scales=xs[:, a:b], in_=src)
-        wq_rest = keep.tile([P, 3 * P], U32, name="wq_rest", tag="wraw2", align_bytes=64)
+        wq_rest = placed.tile([P, 3 * P], U32, name="wq_rest", align_bytes=64, offset=0)
         nc.vector.quantize_mx(out=wq_rest[:, 0:P].bitcast(FP8X4), scales=ws[:, P : 2 * P], in_=wg[:, 512:1024])
         nc.vector.quantize_mx(out=wq_rest[:, P : 3 * P].bitcast(FP8X4), scales=ws[:, 2 * P : 4 * P], in_=wg[:, 1024:2048])
 
@@ -145,13 +153,13 @@ def tile_picked_treeup_gelu_e_kernel(tc, xT, w1, w2_words, w2_scales, share, off
         for t in range(4):
             wq = (wq_first[:] if t == 0 else wq_rest[:, P * (t - 1) : P * t]).bitcast(FP8X4)
             if t == 0:
-                for (a, b), i in zip(steps, (0, 1, 2, 3, 4)):
+                for (a, b), i in zip(steps, (3, 4, 0, 1, 2)):
                     acc = bank(i)[:, 0 : b - a]
                     nc.tensor.matmul_mx(out=acc, lhsT=wq, lhsT_scale=ws[:, 0:P], rhs=xq(a, b), rhs_scale=xs[:, a:b], start=True, stop=True)
                     nc.scalar.activation(out=h[0][:, a:b], in_=acc, func=GELU)
             else:
                 accs = [bank(i) for i in ((5, 6), (7, 3), (4, 5))[t - 1]]
-                for a, b in spans([512, 512]):
+                for a, b in spans([256, 256, 512]):
                     nc.tensor.matmul_mx(out=accs[a // 512][:, a % 512 : a % 512 + b - a], lhsT=wq, lhsT_scale=ws[:, P * t : P * t + P],
                                         rhs=xq(a, b), rhs_scale=xs[:, a:b], start=True, stop=True)
                     if b % 512 == 0:

@@ -101,7 +101,7 @@ def tile_picked_treeup_gelu_e_kernel(tc, xT, w1, w2_words, w2_scales, share, off
         warm_s = keep.tile([P, 512], U8, name="warm_s", align_bytes=64)
         nc.vector.quantize_mx(out=warm_q[:].bitcast(FP8X4), scales=warm_s[:], in_=pairs[0][:, 0:2048])
         spare = bank(7)
-        nc.tensor.transpose(spare[:, 0:P], wraw[0][:, 0, 0:P], ident[:])
+        nc.tensor.transpose(spare[:, 0:P], wraw[1][:, 0, 0:P], ident[:])
         for i in range(3):
             nc.tensor.matmul_mx(out=spare[:], lhsT=warm_q[:, 0:P].bitcast(FP8X4), lhsT_scale=warm_s[:, 0:P], rhs=warm_q[:].bitcast(FP8X4), rhs_scale=warm_s[:],
                                 start=True, stop=True)

@@ -19,8 +19,8 @@ MULT = mybir.AluOpType.mult
 ADD = mybir.AluOpType.add
 
 P = 128
-X0 = [1024,512,512]
-X1 = [768,768,256,256]
+X0 = [1280, 768]
+X1 = [768, 768, 256, 128, 128]
 
 
 def spans(widths, start=0):
@@ -87,16 +87,18 @@ def tile_picked_treeup_gelu_e_kernel(tc, xT, w1, w2_words, w2_scales, share, off
             else:
                 nc.scalar.copy(out=dst, in_=src)
 
-        rows = [keep.tile([P, 2, 256], U32, name="rows%d" % q, align_bytes=64) for q in range(3)]
-        xg_d = keep.tile([P, 512], U32, name="xg_d", align_bytes=64)
+        rows = [keep.tile([P, 2, 256], U32, name="rows%d" % q, align_bytes=64) for q in range(2)]
+        xg_d = keep.tile([P, 1024], U32, name="xg_d", align_bytes=64)
 
         def pick(u):
             window = pairs[u][:].bitcast(U32)
-            for q in range(3):
+            for q in range(2):
                 nc.vector.tensor_copy(out=rows[q][:, u, :], in_=window.indirect(offs_t[:, 16 * q : 16 * q + 16]))
-            nc.vector.tensor_copy(out=xg_d[:].rearrange("p (s u) -> p s u", u=2)[:, :, u], in_=window.indirect(offs_t[:, 48:64]))
+            for a in (0, 256):
+                nc.vector.tensor_copy(out=xg_d[:].rearrange("p (s u) -> p s u", u=2)[:, a : a + 256, u], in_=window.indirect(offs_t[:, 32 + a // 16 : 48 + a // 16]))
 
-        cast("v", 0, 0, 0, 1024)
+        cast("s", 0, 0, 0, 448)
+        cast("v", 0, 0, 448, 1280)
         warm_q = keep.tile([P, 512], U32, name="warm_q", align_bytes=64)
         warm_s = keep.tile([P, 512], U8, name="warm_s", align_bytes=64)
         nc.vector.quantize_mx(out=warm_q[:].bitcast(FP8X4), scales=warm_s[:], in_=pairs[0][:, 0:2048])
@@ -105,16 +107,16 @@ def tile_picked_treeup_gelu_e_kernel(tc, xT, w1, w2_words, w2_scales, share, off
         for i in range(3):
             nc.tensor.matmul_mx(out=spare[:], lhsT=warm_q[:, 0:P].bitcast(FP8X4), lhsT_scale=warm_s[:, 0:P], rhs=warm_q[:].bitcast(FP8X4), rhs_scale=warm_s[:],
                                 start=True, stop=True)
-        cast("s", 0, 1024, 1024, 1536)
-        cast("v", 0, 1536, 1536, 1888)
-        cast("s", 0, 1536, 1888, 2048)
+        cast("v", 0, 1280, 1280, 1792)
+        cast("s", 0, 1280, 1792, 2048)
         pick(0)
         cast("s", 1, 0, 0, 768)
-        cast("s", 1, 768, 768, 1216)
-        cast("v", 1, 768, 1216, 1536)
+        cast("s", 1, 768, 768, 1088)
+        cast("v", 1, 768, 1088, 1536)
         cast("v", 1, 1536, 1536, 1792)
-        cast("v", 1, 1792, 1792, 1968)
-        cast("s", 1, 1792, 1968, 2048)
+        cast("s", 1, 1792, 1792, 1920)
+        cast("v", 1, 1920, 1920, 2016)
+        cast("s", 1, 1920, 2016, 2048)
 
         wg = keep.tile([P, 4 * H], BF16, name="wg", align_bytes=64)
         for hh in range(4):
@@ -124,11 +126,10 @@ def tile_picked_treeup_gelu_e_kernel(tc, xT, w1, w2_words, w2_scales, share, off
                 nc.scalar.copy(out=dst[:, :, :, a:b], in_=src[:, :, :, a:b])
 
         pick(1)
-        xg_a = keep.tile([P, 1024], U32, name="xg_a", align_bytes=64)
+        xg_a = keep.tile([P, 512], U32, name="xg_a", align_bytes=64)
         xg_c = placed.tile([P, 512], U32, name="xg_c", align_bytes=64, offset=0)
-        for q in range(2):
-            nc.gpsimd.tensor_copy(out=xg_a[:, 512 * q : 512 * q + 512].rearrange("p (s u) -> p s u", u=2), in_=rows[q][:].rearrange("p u s -> p s u"))
-        nc.scalar.copy(out=xg_c[:].rearrange("p (c i u) -> p c u i", i=4, u=2), in_=rows[2][:].rearrange("p u (c i) -> p c u i", i=4))
+        nc.gpsimd.tensor_copy(out=xg_a[:].rearrange("p (s u) -> p s u", u=2), in_=rows[0][:].rearrange("p u s -> p s u"))
+        nc.scalar.copy(out=xg_c[:].rearrange("p (c i u) -> p c u i", i=4, u=2), in_=rows[1][:].rearrange("p u (c i) -> p c u i", i=4))
         xs = keep.tile([P, S], U8, name="xs", align_bytes=64)
         xq_first = keep.tile([P, 256], U32, name="xq_first", align_bytes=64)
         xq_t = placed.tile([P, S - 256], U32, name="xq_t", align_bytes=64, offset=2048)
@@ -138,10 +139,10 @@ def tile_picked_treeup_gelu_e_kernel(tc, xT, w1, w2_words, w2_scales, share, off
         def xq(a, b):
             return (xq_first[:, a:b] if a < 256 else xq_t[:, a - 256 : b - 256]).bitcast(FP8X4)
 
-        steps = [(0, 256), (256, 512), (768, S), (512, 640), (640, 768)]
+        steps = [(0, 256), (512, 768), (768, S), (256, 384), (384, 512)]
         nc.vector.quantize_mx(out=wq_first[:].bitcast(FP8X4), scales=ws[:, 0:P], in_=wg[:, 0:512])
         for a, b in steps:
-            part, first = (xg_a, 0) if a < 512 else (xg_c, 512) if a < 768 else (xg_d, 768)
+            part, first = (xg_a, 0) if a < 256 else (xg_c, 256) if a < 512 else (xg_d, 512)
             src = part[:].bitcast(BF16)[:, 4 * (a - first) : 4 * (b - first)]
             nc.vector.quantize_mx(out=xq(a, b), scales=xs[:, a:b], in_=src)
         wq_rest = placed.tile([P, 3 * P], U32, name="wq_rest", align_bytes=64, offset=0)

@@ -35,7 +35,6 @@ def tile_picked_treeup_gelu_e_kernel(tc, xT, w1, w2_words, w2_scales, share, off
     nc = tc.nc
     with ExitStack() as ctx:
         keep = ctx.enter_context(tc.tile_pool(name="keep", bufs=1))
-        placed = ctx.enter_context(tc.tile_pool(name="placed", bufs=1))
         psum = ctx.enter_context(tc.psum_pool(name="psum", bufs=1))
 
         def bank(i):
@@ -62,10 +61,7 @@ def tile_picked_treeup_gelu_e_kernel(tc, xT, w1, w2_words, w2_scales, share, off
         w4 = w1.rearrange("(p j) c -> p j c", j=4)
         wraw = []
         for hh in range(4):
-            if hh < 3:
-                wraw.append(keep.tile([P, 4, P], F32, name="wraw%d" % hh, align_bytes=64))
-            else:
-                wraw.append(placed.tile([P, 4, P], F32, name="wraw3", align_bytes=64, offset=1024))
+            wraw.append(keep.tile([P, 4, P], F32, name="wraw%d" % hh, align_bytes=64))
             nc.sync.dma_start(wraw[hh][:], w4[:, :, P * hh : P * hh + P])
         nc.sync.dma_start(par_t[:], par)
         share_t = []
@@ -87,15 +83,14 @@ def tile_picked_treeup_gelu_e_kernel(tc, xT, w1, w2_words, w2_scales, share, off
             else:
                 nc.scalar.copy(out=dst, in_=src)
 
-        rows = [keep.tile([P, 2, 256], U32, name="rows%d" % q, align_bytes=64) for q in range(2)]
-        xg_d = keep.tile([P, 1024], U32, name="xg_d", align_bytes=64)
+        rows = [keep.tile([P, 2, 256], U32, name="rows%d" % q, align_bytes=64) for q in range(3)]
+        xg_d = keep.tile([P, 512], U32, name="xg_d", align_bytes=64)
 
         def pick(u):
             window = pairs[u][:].bitcast(U32)
-            for q in range(2):
+            for q in range(3):
                 nc.vector.tensor_copy(out=rows[q][:, u, :], in_=window.indirect(offs_t[:, 16 * q : 16 * q + 16]))
-            for a in (0, 256):
-                nc.vector.tensor_copy(out=xg_d[:].rearrange("p (s u) -> p s u", u=2)[:, a : a + 256, u], in_=window.indirect(offs_t[:, 32 + a // 16 : 48 + a // 16]))
+            nc.vector.tensor_copy(out=xg_d[:].rearrange("p (s u) -> p s u", u=2)[:, :, u], in_=window.indirect(offs_t[:, 48:64]))
 
         cast("s", 0, 0, 0, 448)
         cast("v", 0, 0, 448, 1280)
@@ -119,33 +114,39 @@ def tile_picked_treeup_gelu_e_kernel(tc, xT, w1, w2_words, w2_scales, share, off
         cast("s", 1, 1920, 2016, 2048)
 
         wg = keep.tile([P, 4 * H], BF16, name="wg", align_bytes=64)
-        for hh in range(4):
-            dst = wg[:].rearrange("p (t m j) -> p m j t", t=4, j=4)[:, 32 * hh : 32 * hh + 32, :, :]
-            src = wraw[hh][:].rearrange("p j (m t) -> p m j t", t=4)
-            for a, b in spans([4] if hh < 3 else [2, 2]):
-                nc.scalar.copy(out=dst[:, :, :, a:b], in_=src[:, :, :, a:b])
+
+        def deal(hh, a, b):
+            dst = wg[:].rearrange("p (t m j) -> p m j t", t=4, j=4)[:, 32 * hh : 32 * hh + 32, :, a:b]
+            nc.scalar.copy(out=dst, in_=wraw[hh][:].rearrange("p j (m t) -> p m j t", t=4)[:, :, :, a:b])
+
+        for hh in range(3):
+            deal(hh, 0, 4)
+        deal(3, 0, 2)
 
         pick(1)
         xg_a = keep.tile([P, 512], U32, name="xg_a", align_bytes=64)
-        xg_c = placed.tile([P, 512], U32, name="xg_c", align_bytes=64, offset=0)
+        xg_c = keep.tile([P, 1024], U32, name="xg_c", tag="wraw2", align_bytes=64)
         nc.gpsimd.tensor_copy(out=xg_a[:].rearrange("p (s u) -> p s u", u=2), in_=rows[0][:].rearrange("p u s -> p s u"))
-        nc.scalar.copy(out=xg_c[:].rearrange("p (c i u) -> p c u i", i=4, u=2), in_=rows[1][:].rearrange("p u (c i) -> p c u i", i=4))
+        for q in range(2):
+            nc.scalar.copy(out=xg_c[:, 512 * q : 512 * q + 512].rearrange("p (c i u) -> p c u i", i=4, u=2),
+                           in_=rows[1 + q][:].rearrange("p u (c i) -> p c u i", i=4))
+        deal(3, 2, 4)
         xs = keep.tile([P, S], U8, name="xs", align_bytes=64)
         xq_first = keep.tile([P, 256], U32, name="xq_first", align_bytes=64)
-        xq_t = placed.tile([P, S - 256], U32, name="xq_t", align_bytes=64, offset=2048)
+        xq_t = keep.tile([P, S - 256], U32, name="xq_t", tag="rows1", align_bytes=64)
         ws = keep.tile([P, H], U8, name="ws", align_bytes=64)
         wq_first = keep.tile([P, P], U32, name="wq_first", align_bytes=64)
 
         def xq(a, b):
             return (xq_first[:, a:b] if a < 256 else xq_t[:, a - 256 : b - 256]).bitcast(FP8X4)
 
-        steps = [(0, 256), (512, 768), (768, S), (256, 384), (384, 512)]
+        steps = [(0, 256), (768, S), (256, 512), (512, 640), (640, 768)]
         nc.vector.quantize_mx(out=wq_first[:].bitcast(FP8X4), scales=ws[:, 0:P], in_=wg[:, 0:512])
         for a, b in steps:
-            part, first = (xg_a, 0) if a < 256 else (xg_c, 256) if a < 512 else (xg_d, 512)
+            part, first = (xg_a, 0) if a < 256 else (xg_c, 256) if a < 768 else (xg_d, 768)
             src = part[:].bitcast(BF16)[:, 4 * (a - first) : 4 * (b - first)]
             nc.vector.quantize_mx(out=xq(a, b), scales=xs[:, a:b], in_=src)
-        wq_rest = placed.tile([P, 3 * P], U32, name="wq_rest", align_bytes=64, offset=0)
+        wq_rest = keep.tile([P, 3 * P], U32, name="wq_rest", tag="wraw2", align_bytes=64)
         nc.vector.quantize_mx(out=wq_rest[:, 0:P].bitcast(FP8X4), scales=ws[:, P : 2 * P], in_=wg[:, 512:1024])
         nc.vector.quantize_mx(out=wq_rest[:, P : 3 * P].bitcast(FP8X4), scales=ws[:, 2 * P : 4 * P], in_=wg[:, 1024:2048])
 

@@ -15,12 +15,13 @@ U8 = mybir.dt.uint8
 FP8X4 = mybir.dt.float8_e4m3fn_x4
 FP4X4 = mybir.dt.float4_e2m1fn_x4
 GELU = mybir.ActivationFunctionType.Gelu_apprx_tanh
+COPY = mybir.ActivationFunctionType.Copy
 MULT = mybir.AluOpType.mult
 ADD = mybir.AluOpType.add
 
 P = 128
-X0 = [1280, 768]
-X1 = [768, 768, 256, 128, 128]
+BY_VECTOR = 640
+BY_SCALAR = S - BY_VECTOR
 
 
 def spans(widths, start=0):
@@ -51,13 +52,12 @@ def tile_picked_treeup_gelu_e_kernel(tc, xT, w1, w2_words, w2_scales, share, off
         make_identity(nc, ident[:])
 
         x4 = xT.rearrange("(p j) t -> p j t", j=4)
-        raw = {}
-        for u, widths in enumerate((X0, X1)):
-            for a, b in spans(widths):
-                raw[u, a] = keep.tile([P, 2, b - a], F32, name="raw%d_%d" % (u, a))
-                nc.sync.dma_start(raw[u, a][:], x4[:, 2 * u : 2 * u + 2, a:b])
-                if (u, a) == (0, 0):
-                    nc.sync.dma_start(offs_t[:], offs)
+        raw = []
+        for j in range(4):
+            raw.append(keep.tile([P, T], F32, name="raw%d" % j))
+            nc.sync.dma_start(raw[j][:], x4[:, j, :])
+            if j == 0:
+                nc.sync.dma_start(offs_t[:], offs)
         w4 = w1.rearrange("(p j) c -> p j c", j=4)
         wraw = []
         for hh in range(4):
@@ -73,45 +73,26 @@ def tile_picked_treeup_gelu_e_kernel(tc, xT, w1, w2_words, w2_scales, share, off
         for q in range(4):
             nc.sync.dma_start(w2s[32 * q : 32 * q + 4, :].bitcast(I32), w2_scales[0, 4 * q : 4 * q + 4, :].bitcast(I32))
 
-        pairs = [keep.tile([P, 2 * T], BF16, name="pairs%d" % u, align_bytes=64) for u in range(2)]
+        rows = keep.tile([P, 4, BY_SCALAR], BF16, name="rows", align_bytes=64)
+        xg_s = keep.tile([P, 4 * BY_SCALAR], BF16, name="xg_s", align_bytes=64)
+        xg_v = keep.tile([P, 4 * BY_VECTOR], BF16, name="xg_v", align_bytes=64)
 
-        def cast(engine, u, first, a, b):
-            dst = pairs[u][:, 2 * a : 2 * b].rearrange("p (c i e) -> p c e i", i=4, e=2)
-            src = raw[u, first][:, :, a - first : b - first].rearrange("p e (c i) -> p c e i", i=4)
-            if engine == "v":
-                nc.vector.tensor_copy(out=dst, in_=src)
-            else:
-                nc.scalar.copy(out=dst, in_=src)
+        def pick_scalar(j, a, b):
+            nc.scalar.activation(out=rows[:, j, a:b], in_=raw[j][:].indirect(offs_t[:, (BY_VECTOR + a) // 16 : (BY_VECTOR + b) // 16]), func=COPY)
 
-        rows = [keep.tile([P, 2, 256], U32, name="rows%d" % q, align_bytes=64) for q in range(3)]
-        xg_d = keep.tile([P, 512], U32, name="xg_d", align_bytes=64)
+        def lay(u, a, b):
+            nc.gpsimd.tensor_copy(out=xg_s[:].rearrange("p (s j) -> p s j", j=4)[:, a:b, 2 * u : 2 * u + 2],
+                                  in_=rows[:, 2 * u : 2 * u + 2, a:b].rearrange("p e s -> p s e"))
 
-        def pick(u):
-            window = pairs[u][:].bitcast(U32)
-            for q in range(3):
-                nc.vector.tensor_copy(out=rows[q][:, u, :], in_=window.indirect(offs_t[:, 16 * q : 16 * q + 16]))
-            nc.vector.tensor_copy(out=xg_d[:].rearrange("p (s u) -> p s u", u=2)[:, :, u], in_=window.indirect(offs_t[:, 48:64]))
-
-        cast("s", 0, 0, 0, 448)
-        cast("v", 0, 0, 448, 1280)
-        warm_q = keep.tile([P, 512], U32, name="warm_q", align_bytes=64)
-        warm_s = keep.tile([P, 512], U8, name="warm_s", align_bytes=64)
-        nc.vector.quantize_mx(out=warm_q[:].bitcast(FP8X4), scales=warm_s[:], in_=pairs[0][:, 0:2048])
-        spare = bank(7)
-        nc.tensor.transpose(spare[:, 0:P], wraw[1][:, 0, 0:P], ident[:])
-        for i in range(3):
-            nc.tensor.matmul_mx(out=spare[:], lhsT=warm_q[:, 0:P].bitcast(FP8X4), lhsT_scale=warm_s[:, 0:P], rhs=warm_q[:].bitcast(FP8X4), rhs_scale=warm_s[:],
-                                start=True, stop=True)
-        cast("v", 0, 1280, 1280, 1792)
-        cast("s", 0, 1280, 1792, 2048)
-        pick(0)
-        cast("s", 1, 0, 0, 768)
-        cast("s", 1, 768, 768, 1088)
-        cast("v", 1, 768, 1088, 1536)
-        cast("v", 1, 1536, 1536, 1792)
-        cast("s", 1, 1792, 1792, 1920)
-        cast("v", 1, 1920, 1920, 2016)
-        cast("s", 1, 1920, 2016, 2048)
+        for j in range(4):
+            nc.vector.tensor_copy(out=xg_v[:].rearrange("p (s j) -> p s j", j=4)[:, :, j], in_=raw[j][:].indirect(offs_t[:, 0 : BY_VECTOR // 16]))
+            if j < 3:
+                pick_scalar(j, 0, BY_SCALAR)
+            if j == 1:
+                lay(0, 0, BY_SCALAR)
+        for a, b in spans([P, BY_SCALAR - P]):
+            pick_scalar(3, a, b)
+            lay(1, a, b)
 
         wg = keep.tile([P, 4 * H], BF16, name="wg", align_bytes=64)
 
@@ -121,48 +102,46 @@ def tile_picked_treeup_gelu_e_kernel(tc, xT, w1, w2_words, w2_scales, share, off
 
         for hh in range(3):
             deal(hh, 0, 4)
-        deal(3, 0, 2)
+        deal(3, 0, 1)
+        deal(3, 1, 4)
 
-        pick(1)
-        xg_a = keep.tile([P, 512], U32, name="xg_a", align_bytes=64)
-        xg_c = keep.tile([P, 1024], U32, name="xg_c", tag="wraw2", align_bytes=64)
-        nc.gpsimd.tensor_copy(out=xg_a[:].rearrange("p (s u) -> p s u", u=2), in_=rows[0][:].rearrange("p u s -> p s u"))
-        for q in range(2):
-            nc.scalar.copy(out=xg_c[:, 512 * q : 512 * q + 512].rearrange("p (c i u) -> p c u i", i=4, u=2),
-                           in_=rows[1 + q][:].rearrange("p u (c i) -> p c u i", i=4))
-        deal(3, 2, 4)
         xs = keep.tile([P, S], U8, name="xs", align_bytes=64)
-        xq_first = keep.tile([P, 256], U32, name="xq_first", align_bytes=64)
-        xq_t = keep.tile([P, S - 256], U32, name="xq_t", tag="rows1", align_bytes=64)
+        xq_v = keep.tile([P, BY_VECTOR], U32, name="xq_v", align_bytes=64)
+        xq_s = keep.tile([P, BY_SCALAR], U32, name="xq_s", tag="wraw3", align_bytes=64)
         ws = keep.tile([P, H], U8, name="ws", align_bytes=64)
-        wq_first = keep.tile([P, P], U32, name="wq_first", align_bytes=64)
+        wq = keep.tile([P, H], U32, name="wq", align_bytes=64)
 
         def xq(a, b):
-            return (xq_first[:, a:b] if a < 256 else xq_t[:, a - 256 : b - 256]).bitcast(FP8X4)
+            return (xq_v[:, a:b] if a < BY_VECTOR else xq_s[:, a - BY_VECTOR : b - BY_VECTOR]).bitcast(FP8X4)
 
-        steps = [(0, 256), (768, S), (256, 512), (512, 640), (640, 768)]
-        nc.vector.quantize_mx(out=wq_first[:].bitcast(FP8X4), scales=ws[:, 0:P], in_=wg[:, 0:512])
-        for a, b in steps:
-            part, first = (xg_a, 0) if a < 256 else (xg_c, 256) if a < 768 else (xg_d, 768)
-            src = part[:].bitcast(BF16)[:, 4 * (a - first) : 4 * (b - first)]
-            nc.vector.quantize_mx(out=xq(a, b), scales=xs[:, a:b], in_=src)
-        wq_rest = keep.tile([P, 3 * P], U32, name="wq_rest", tag="wraw2", align_bytes=64)
-        nc.vector.quantize_mx(out=wq_rest[:, 0:P].bitcast(FP8X4), scales=ws[:, P : 2 * P], in_=wg[:, 512:1024])
-        nc.vector.quantize_mx(out=wq_rest[:, P : 3 * P].bitcast(FP8X4), scales=ws[:, 2 * P : 4 * P], in_=wg[:, 1024:2048])
+        def quant_x(a, b):
+            part, first = (xg_v, 0) if a < BY_VECTOR else (xg_s, BY_VECTOR)
+            nc.vector.quantize_mx(out=xq(a, b), scales=xs[:, a:b], in_=part[:, 4 * (a - first) : 4 * (b - first)])
+
+        def quant_w(a, b):
+            nc.vector.quantize_mx(out=wq[:, P * a : P * b].bitcast(FP8X4), scales=ws[:, P * a : P * b], in_=wg[:, 512 * a : 512 * b])
+
+        quant_x(0, 512)
+        quant_x(512, 640)
+        quant_w(0, 1)
+        quant_x(768, S)
+        quant_x(640, 768)
+        quant_w(1, 2)
+        quant_w(2, 4)
 
         h = [keep.tile([P, S], F32, name="h%d" % t, align_bytes=64) for t in range(4)]
         hd = keep.tile([P, 4, 256], F32, name="hd")
         for t in range(4):
-            wq = (wq_first[:] if t == 0 else wq_rest[:, P * (t - 1) : P * t]).bitcast(FP8X4)
+            lhs = wq[:, P * t : P * t + P].bitcast(FP8X4)
             if t == 0:
-                for (a, b), i in zip(steps, (3, 4, 0, 1, 2)):
+                for (a, b), i in zip(((512, 640), (0, 256), (256, 512), (768, S), (640, 768)), (3, 4, 0, 1, 2)):
                     acc = bank(i)[:, 0 : b - a]
-                    nc.tensor.matmul_mx(out=acc, lhsT=wq, lhsT_scale=ws[:, 0:P], rhs=xq(a, b), rhs_scale=xs[:, a:b], start=True, stop=True)
+                    nc.tensor.matmul_mx(out=acc, lhsT=lhs, lhsT_scale=ws[:, 0:P], rhs=xq(a, b), rhs_scale=xs[:, a:b], start=True, stop=True)
                     nc.scalar.activation(out=h[0][:, a:b], in_=acc, func=GELU)
             else:
                 accs = [bank(i) for i in ((5, 6), (7, 3), (4, 5))[t - 1]]
-                for a, b in spans([256, 256, 512]):
-                    nc.tensor.matmul_mx(out=accs[a // 512][:, a % 512 : a % 512 + b - a], lhsT=wq, lhsT_scale=ws[:, P * t : P * t + P],
+                for a, b in spans([512, P, P, 256]):
+                    nc.tensor.matmul_mx(out=accs[a // 512][:, a % 512 : a % 512 + b - a], lhsT=lhs, lhsT_scale=ws[:, P * t : P * t + P],
                                         rhs=xq(a, b), rhs_scale=xs[:, a:b], start=True, stop=True)
                     if b % 512 == 0:
                         nc.scalar.activation(out=h[t][:, b - 512 : b], in_=accs[a // 512][:], func=GELU)

@@ -102,8 +102,8 @@ def tile_picked_treeup_gelu_e_kernel(tc, xT, w1, w2_words, w2_scales, share, off
 
         for hh in range(3):
             deal(hh, 0, 4)
-        deal(3, 0, 1)
-        deal(3, 1, 4)
+        deal(3, 0, 2)
+        deal(3, 2, 4)
 
         xs = keep.tile([P, S], U8, name="xs", align_bytes=64)
         xq_v = keep.tile([P, BY_VECTOR], U32, name="xq_v", align_bytes=64)
@@ -124,9 +124,9 @@ def tile_picked_treeup_gelu_e_kernel(tc, xT, w1, w2_words, w2_scales, share, off
         quant_x(0, 512)
         quant_x(512, 640)
         quant_w(0, 1)
+        quant_w(1, 2)
         quant_x(768, S)
         quant_x(640, 768)
-        quant_w(1, 2)
         quant_w(2, 4)
 
         h = [keep.tile([P, S], F32, name="h%d" % t, align_bytes=64) for t in range(4)]
@@ -134,12 +134,12 @@ def tile_picked_treeup_gelu_e_kernel(tc, xT, w1, w2_words, w2_scales, share, off
         for t in range(4):
             lhs = wq[:, P * t : P * t + P].bitcast(FP8X4)
             if t == 0:
-                for (a, b), i in zip(((512, 640), (0, 256), (256, 512), (768, S), (640, 768)), (3, 4, 0, 1, 2)):
+                for (a, b), i in zip(((0, P), (P, 384), (384, 640), (768, S), (640, 768)), (3, 4, 5, 1, 2)):
                     acc = bank(i)[:, 0 : b - a]
                     nc.tensor.matmul_mx(out=acc, lhsT=lhs, lhsT_scale=ws[:, 0:P], rhs=xq(a, b), rhs_scale=xs[:, a:b], start=True, stop=True)
                     nc.scalar.activation(out=h[0][:, a:b], in_=acc, func=GELU)
             else:
-                accs = [bank(i) for i in ((5, 6), (7, 3), (4, 5))[t - 1]]
+                accs = [bank(i) for i in ((5, 4), (6, 7), (3, 5))[t - 1]]
                 for a, b in spans([512, P, P, 256]):
                     nc.tensor.matmul_mx(out=accs[a // 512][:, a % 512 : a % 512 + b - a], lhsT=lhs, lhsT_scale=ws[:, P * t : P * t + P],
                                         rhs=xq(a, b), rhs_scale=xs[:, a:b], start=True, stop=True)
@@ -197,7 +197,7 @@ def tile_picked_treeup_gelu_e_kernel(tc, xT, w1, w2_words, w2_scales, share, off
                 nc.scalar.copy(out=res[:], in_=acc)
                 nc.sync.dma_start(out[P * mb : P * mb + P, a : a + 256], res[:])
 
-        sums = [[bank(0), bank(1), bank(2)], [bank(6), bank(7), bank(3)]]
+        sums = [[bank(1), bank(2), bank(0)], [bank(4), bank(6), bank(7)]]
         g = keep.tile([P, 4, 768], F32, name="g")
 
         def turn_all(src, t, **flag):
@@ -215,7 +215,7 @@ def tile_picked_treeup_gelu_e_kernel(tc, xT, w1, w2_words, w2_scales, share, off
         follow(g[:, 1, 512:768], 1, 512, 768)
         turn_all(g[:, 1, :], 1, last=True)
         zt = [round_sums(sums[0][q], "zt0%d" % q) for q in range(3)]
-        backs = [bank(4), bank(5)]
+        backs = [bank(3), bank(5)]
         follow(g[:, 2, 0:512], 2, 0, 512)
         follow(g[:, 2, 512:768], 2, 512, 768)
         turn_all(g[:, 2, :], 2)
@@ -225,7 +225,7 @@ def tile_picked_treeup_gelu_e_kernel(tc, xT, w1, w2_words, w2_scales, share, off
             if q < 2:
                 turn_back(backs[q], 0, zt[q])
         turn_back(backs[0], 1, round_sums(sums[1][0], "zt10"))
-        backs.append(bank(6))
+        backs.append(bank(4))
         turn_back(backs[2], 0, zt[2])
         for q in (1, 2):
             turn_back(backs[q], 1, round_sums(sums[1][q], "zt1%d" % q))
@@ -236,14 +236,14 @@ def tile_picked_treeup_gelu_e_kernel(tc, xT, w1, w2_words, w2_scales, share, off
         for t in range(4):
             follow(gd[:, t, :], t, 768, S)
         finish_by_scalar(quant_z([part[:] for part in zg0], "0"), 0, (1, 2))
-        finish_by_scalar(quant_z([zg1[:]], "1"), 256, (3, 4))
+        finish_by_scalar(quant_z([zg1[:]], "1"), 256, (7, 3))
         zg_d = []
         for q in range(2):
             zg_d.append(keep.tile([P, 512], BF16, name="zg_d%d" % q, tag=("zg00", "zg1")[q], align_bytes=64))
             add(zg_d[q][:], gd[:, :, P * q : P * q + P], hd[:, :, P * q : P * q + P])
             if q == 0:
-                last = [(product_two_banks(quant_z([zg2[:]], "2"), 256, (0, 7)), 0, 256)]
-        for q, banks in enumerate(((5, 6), (1, 2))):
+                last = [(product_two_banks(quant_z([zg2[:]], "2"), 256, (0, 6)), 0, 256)]
+        for q, banks in enumerate(((5, 4), (1, 2))):
             last.append((product_two_banks(quant_z([zg_d[q][:]], "d%d" % q, slot=("zg2", None)[q]), P, banks), 256 + P * q, 384 + P * q))
         res = [keep.tile([P, 512], F32, name="res_last%d" % mb, tag=("res_last0", "zg1")[mb], align_bytes=64) for mb in range(2)]
         for accs, a, b in last:

@@ -125,8 +125,7 @@ def tile_picked_treeup_gelu_e_kernel(tc, xT, w1, w2_words, w2_scales, share, off
         quant_x(512, 640)
         quant_w(0, 1)
         quant_w(1, 2)
-        quant_x(768, S)
-        quant_x(640, 768)
+        quant_x(BY_VECTOR, S)
         quant_w(2, 4)
 
         h = [keep.tile([P, S], F32, name="h%d" % t, align_bytes=64) for t in range(4)]
@@ -191,12 +190,6 @@ def tile_picked_treeup_gelu_e_kernel(tc, xT, w1, w2_words, w2_scales, share, off
                 second(accs[mb], mb, *z)
             return accs
 
-        def finish_by_scalar(z, a, banks):
-            for mb, acc in enumerate(product_two_banks(z, 256, banks)):
-                res = keep.tile([P, 256], F32, name="res%d_%d" % (a, mb))
-                nc.scalar.copy(out=res[:], in_=acc)
-                nc.sync.dma_start(out[P * mb : P * mb + P, a : a + 256], res[:])
-
         sums = [[bank(1), bank(2), bank(0)], [bank(4), bank(6), bank(7)]]
         g = keep.tile([P, 4, 768], F32, name="g")
 
@@ -215,6 +208,9 @@ def tile_picked_treeup_gelu_e_kernel(tc, xT, w1, w2_words, w2_scales, share, off
         follow(g[:, 1, 512:768], 1, 512, 768)
         turn_all(g[:, 1, :], 1, last=True)
         zt = [round_sums(sums[0][q], "zt0%d" % q) for q in range(3)]
+        plain = keep.tile([P, 2, 256], F32, name="plain")
+        for t in range(2):
+            nc.scalar.activation(out=plain[:, t, :], in_=h[t][:].indirect(par_t[:, 48:64]), func=COPY)
         backs = [bank(3), bank(5)]
         follow(g[:, 2, 0:512], 2, 0, 512)
         follow(g[:, 2, 512:768], 2, 512, 768)
@@ -231,24 +227,41 @@ def tile_picked_treeup_gelu_e_kernel(tc, xT, w1, w2_words, w2_scales, share, off
             turn_back(backs[q], 1, round_sums(sums[1][q], "zt1%d" % q))
         zg0 = [weave(backs[0][:, 256 * c : 256 * c + 256], 1, "zg0%d" % c) for c in range(2)]
         zg1 = weave(backs[1][:], 2, "zg1")
-        zg2 = weave(backs[2][:], 2, "zg2")
+        zg2 = [weave(backs[2][:, 256 * c : 256 * c + 256], 1, "zg2%d" % c) for c in range(2)]
         gd = keep.tile([P, 4, 256], F32, name="gd", tag="share0", align_bytes=64)
-        for t in range(4):
+        nc.vector.tensor_tensor(out=gd[:, 0:2, :], in0=plain[:], in1=share_t[1][:, 256:512].unsqueeze(1).to_broadcast([P, 2, 256]), op=MULT)
+        for t in range(2, 4):
             follow(gd[:, t, :], t, 768, S)
-        finish_by_scalar(quant_z([part[:] for part in zg0], "0"), 0, (1, 2))
-        finish_by_scalar(quant_z([zg1[:]], "1"), 256, (7, 3))
-        zg_d = []
-        for q in range(2):
-            zg_d.append(keep.tile([P, 512], BF16, name="zg_d%d" % q, tag=("zg00", "zg1")[q], align_bytes=64))
-            add(zg_d[q][:], gd[:, :, P * q : P * q + P], hd[:, :, P * q : P * q + P])
-            if q == 0:
-                last = [(product_two_banks(quant_z([zg2[:]], "2"), 256, (0, 6)), 0, 256)]
-        for q, banks in enumerate(((5, 4), (1, 2))):
-            last.append((product_two_banks(quant_z([zg_d[q][:]], "d%d" % q, slot=("zg2", None)[q]), P, banks), 256 + P * q, 384 + P * q))
-        res = [keep.tile([P, 512], F32, name="res_last%d" % mb, tag=("res_last0", "zg1")[mb], align_bytes=64) for mb in range(2)]
-        for accs, a, b in last:
-            nc.scalar.copy(out=res[0][:, a:b], in_=accs[0])
-            nc.vector.tensor_copy(out=res[1][:, a:b], in_=accs[1])
-            if b % 256 == 0:
-                (nc.scalar if b == 512 else nc.sync).dma_start(out[0:P, 256 + b : 512 + b], res[0][:, b - 256 : b])
-                nc.sync.dma_start(out[P : 2 * P, 256 + b : 512 + b], res[1][:, b - 256 : b])
+        out3 = out.rearrange("(mb p) s -> p mb s", mb=2)
+
+        def finish_by_halves(z, a, banks):
+            for mb, acc in enumerate(product_two_banks(z, 256, banks)):
+                res = keep.tile([P, 256], F32, name="res%d_%d" % (a, mb))
+                nc.scalar.copy(out=res[:], in_=acc)
+                nc.sync.dma_start(out[P * mb : P * mb + P, a : a + 256], res[:])
+
+        def finish(z, a, n, copy, i, tag=None):
+            acc = bank(i)
+            for mb in range(2):
+                second(acc[:, n * mb : n * mb + n], mb, *z)
+            res = keep.tile([P, 2, n], F32, name="res%d" % a, tag=tag or "res%d" % a, align_bytes=64)
+            copy(out=res[:], in_=acc[:, 0 : 2 * n].rearrange("p (mb s) -> p mb s", mb=2))
+            nc.sync.dma_start(out3[:, :, a : a + n], res[:])
+
+        finish_by_halves(quant_z([part[:] for part in zg0], "0"), 0, (1, 2))
+        zg_d = [keep.tile([P, 512], BF16, name="zg_d%d" % q, tag=("zg00", "zg1")[q], align_bytes=64) for q in range(2)]
+        add(zg_d[0][:], gd[:, :, 0:P], hd[:, :, 0:P])
+        finish_by_halves(quant_z([zg1[:]], "1"), 256, (7, 3))
+        z_d0 = quant_z([zg_d[0][:]], "d0")
+        add(zg_d[1][:], gd[:, :, P : 2 * P], hd[:, :, P : 2 * P])
+        z_c0 = quant_z([zg2[0][:]], "c0")
+        z_d1 = quant_z([zg_d[1][:]], "d1")
+        z_c1 = quant_z([zg2[1][:]], "c1")
+        finish(z_d0, 768, P, nc.vector.tensor_copy, 0, tag="zg21")
+        finish(z_c0, 512, P, nc.vector.tensor_copy, 6)
+        finish(z_d1, 896, P, nc.scalar.copy, 5)
+        accs = product_two_banks(z_c1, P, (4, 1))
+        res = keep.tile([P, 2, P], F32, name="res_last")
+        nc.vector.tensor_copy(out=res[:, 0, :], in_=accs[0])
+        nc.scalar.copy(out=res[:, 1, :], in_=accs[1])
+        nc.sync.dma_start(out3[:, :, 640:768], res[:])

@@ -208,18 +208,20 @@ def tile_picked_treeup_gelu_e_kernel(tc, xT, w1, w2_words, w2_scales, share, off
         follow(g[:, 1, 512:768], 1, 512, 768)
         turn_all(g[:, 1, :], 1, last=True)
         zt = [round_sums(sums[0][q], "zt0%d" % q) for q in range(3)]
-        plain = keep.tile([P, 2, 256], F32, name="plain")
-        for t in range(2):
-            nc.scalar.activation(out=plain[:, t, :], in_=h[t][:].indirect(par_t[:, 48:64]), func=COPY)
+        plain = keep.tile([P, 256], F32, name="plain")
+        nc.scalar.activation(out=plain[:], in_=h[0][:].indirect(par_t[:, 48:64]), func=COPY)
         backs = [bank(3), bank(5)]
         follow(g[:, 2, 0:512], 2, 0, 512)
-        follow(g[:, 2, 512:768], 2, 512, 768)
-        turn_all(g[:, 2, :], 2)
+        for q in range(2):
+            turn(sums[1][q], 0, g[:, 2, 256 * q : 256 * q + 256])
         for q in range(3):
             follow(g[:, 3, 256 * q : 256 * q + 256], 3, 256 * q, 256 * q + 256)
-            turn(sums[1][q], 1, g[:, 3, 256 * q : 256 * q + 256], last=True)
+            turn(sums[1][q], 1, g[:, 3, 256 * q : 256 * q + 256], last=q < 2)
             if q < 2:
                 turn_back(backs[q], 0, zt[q])
+        gd = keep.tile([P, 5, 256], F32, name="gd", tag="share0", align_bytes=64)
+        follow(gd[:, 4, :], 2, 512, 768)
+        turn(sums[1][2], 0, gd[:, 4, :], last=True)
         turn_back(backs[0], 1, round_sums(sums[1][0], "zt10"))
         backs.append(bank(4))
         turn_back(backs[2], 0, zt[2])
@@ -228,9 +230,8 @@ def tile_picked_treeup_gelu_e_kernel(tc, xT, w1, w2_words, w2_scales, share, off
         zg0 = [weave(backs[0][:, 256 * c : 256 * c + 256], 1, "zg0%d" % c) for c in range(2)]
         zg1 = weave(backs[1][:], 2, "zg1")
         zg2 = [weave(backs[2][:, 256 * c : 256 * c + 256], 1, "zg2%d" % c) for c in range(2)]
-        gd = keep.tile([P, 4, 256], F32, name="gd", tag="share0", align_bytes=64)
-        nc.vector.tensor_tensor(out=gd[:, 0:2, :], in0=plain[:], in1=share_t[1][:, 256:512].unsqueeze(1).to_broadcast([P, 2, 256]), op=MULT)
-        for t in range(2, 4):
+        nc.vector.tensor_tensor(out=gd[:, 0, :], in0=plain[:], in1=share_t[1][:, 256:512], op=MULT)
+        for t in range(1, 4):
             follow(gd[:, t, :], t, 768, S)
         out3 = out.rearrange("(mb p) s -> p mb s", mb=2)
 
@@ -240,28 +241,28 @@ def tile_picked_treeup_gelu_e_kernel(tc, xT, w1, w2_words, w2_scales, share, off
                 nc.scalar.copy(out=res[:], in_=acc)
                 nc.sync.dma_start(out[P * mb : P * mb + P, a : a + 256], res[:])
 
-        def finish(z, a, n, copy, i, tag=None):
+        def finish(z, a, n, copy, i):
             acc = bank(i)
             for mb in range(2):
                 second(acc[:, n * mb : n * mb + n], mb, *z)
-            res = keep.tile([P, 2, n], F32, name="res%d" % a, tag=tag or "res%d" % a, align_bytes=64)
+            res = keep.tile([P, 2, n], F32, name="res%d" % a)
             copy(out=res[:], in_=acc[:, 0 : 2 * n].rearrange("p (mb s) -> p mb s", mb=2))
             nc.sync.dma_start(out3[:, :, a : a + n], res[:])
 
         finish_by_halves(quant_z([part[:] for part in zg0], "0"), 0, (1, 2))
         zg_d = [keep.tile([P, 512], BF16, name="zg_d%d" % q, tag=("zg00", "zg1")[q], align_bytes=64) for q in range(2)]
-        add(zg_d[0][:], gd[:, :, 0:P], hd[:, :, 0:P])
+        add(zg_d[0][:], gd[:, 0:4, 0:P], hd[:, :, 0:P])
         finish_by_halves(quant_z([zg1[:]], "1"), 256, (7, 3))
         z_d0 = quant_z([zg_d[0][:]], "d0")
-        add(zg_d[1][:], gd[:, :, P : 2 * P], hd[:, :, P : 2 * P])
+        add(zg_d[1][:], gd[:, 0:4, P : 2 * P], hd[:, :, P : 2 * P])
         z_c0 = quant_z([zg2[0][:]], "c0")
         z_d1 = quant_z([zg_d[1][:]], "d1")
         z_c1 = quant_z([zg2[1][:]], "c1")
-        finish(z_d0, 768, P, nc.vector.tensor_copy, 0, tag="zg21")
-        finish(z_c0, 512, P, nc.vector.tensor_copy, 6)
-        finish(z_d1, 896, P, nc.scalar.copy, 5)
+        finish(z_d0, 768, P, nc.scalar.copy, 0)
+        finish(z_c0, 512, P, nc.scalar.copy, 6)
+        finish(z_d1, 896, P, nc.vector.tensor_copy, 5)
         accs = product_two_banks(z_c1, P, (4, 1))
         res = keep.tile([P, 2, P], F32, name="res_last")
-        nc.vector.tensor_copy(out=res[:, 0, :], in_=accs[0])
-        nc.scalar.copy(out=res[:, 1, :], in_=accs[1])
+        nc.scalar.copy(out=res[:, 0, :], in_=accs[0])
+        nc.vector.tensor_copy(out=res[:, 1, :], in_=accs[1])
         nc.sync.dma_start(out3[:, :, 640:768], res[:])

@@ -249,6 +249,7 @@ def tile_picked_treeup_gelu_e_kernel(tc, xT, w1, w2_words, w2_scales, share, off
             copy(out=res[:], in_=acc[:, 0 : 2 * n].rearrange("p (mb s) -> p mb s", mb=2))
             nc.sync.dma_start(out3[:, :, a : a + n], res[:])
 
+        nc.tensor.matmul_mx(out=bank(3)[:], lhsT=wq[:, 0:P].bitcast(FP8X4), lhsT_scale=ws[:, 0:P], rhs=xq(0, 512), rhs_scale=xs[:, 0:512], start=True, stop=True)
         finish_by_halves(quant_z([part[:] for part in zg0], "0"), 0, (1, 2))
         zg_d = [keep.tile([P, 512], BF16, name="zg_d%d" % q, tag=("zg00", "zg1")[q], align_bytes=64) for q in range(2)]
         add(zg_d[0][:], gd[:, 0:4, 0:P], hd[:, :, 0:P])

@@ -97,8 +97,8 @@ def tile_picked_treeup_gelu_e_kernel(tc, xT, w1, w2_words, w2_scales, share, off
         wg = keep.tile([P, 4 * H], BF16, name="wg", align_bytes=64)
 
         def deal(hh, a, b):
-            dst = wg[:].rearrange("p (t m j) -> p m j t", t=4, j=4)[:, 32 * hh : 32 * hh + 32, :, a:b]
-            nc.scalar.copy(out=dst, in_=wraw[hh][:].rearrange("p j (m t) -> p m j t", t=4)[:, :, :, a:b])
+            dst = wg[:].rearrange("p (t m i e) -> p m i t e", t=4, i=2, e=2)[:, 32 * hh : 32 * hh + 32, :, a:b, :]
+            nc.scalar.copy(out=dst, in_=wraw[hh][:].rearrange("p (i e) (m t) -> p m i t e", e=2, t=4)[:, :, :, a:b, :])
 
         for hh in range(3):
             deal(hh, 0, 4)

from contextlib import ExitStack

import concourse.mybir as mybir
from concourse.masks import make_identity

K, T, S, H, N = 512, 2048, 1024, 512, 256
FLOPS = 2 * K * H * S + 2 * H * N * S

F32 = mybir.dt.float32
BF16 = mybir.dt.bfloat16
I32 = mybir.dt.int32
U32 = mybir.dt.uint32
U16 = mybir.dt.uint16
U8 = mybir.dt.uint8
FP8X4 = mybir.dt.float8_e4m3fn_x4
FP4X4 = mybir.dt.float4_e2m1fn_x4
GELU = mybir.ActivationFunctionType.Gelu_apprx_tanh
COPY = mybir.ActivationFunctionType.Copy
MULT = mybir.AluOpType.mult
ADD = mybir.AluOpType.add

P = 128
BY_VECTOR = 640
BY_SCALAR = S - BY_VECTOR


def spans(widths, start=0):
    res = []
    for w in widths:
        res.append((start, start + w))
        start = start + w
    return res


def tile_picked_treeup_gelu_e_kernel(tc, xT, w1, w2_words, w2_scales, share, offs, par, out):
    nc = tc.nc
    with ExitStack() as ctx:
        keep = ctx.enter_context(tc.tile_pool(name="keep", bufs=1))
        psum = ctx.enter_context(tc.psum_pool(name="psum", bufs=1))

        def bank(i):
            return psum.tile([P, 512], F32, name="bank%d" % i)

        offs_t = keep.tile([P, S // 16], U16, name="offs_t")
        par_t = keep.tile([P, S // 16], U16, name="par_t")

        w2s = keep.tile([P, N], U8, name="w2s", align_bytes=64)
        nc.gpsimd.memset(w2s[:].bitcast(I32), 0)
        warm = keep.tile([P, 1], F32, name="warm")
        nc.scalar.activation(out=warm[:], in_=w2s[:].bitcast(F32)[:, 0:1], func=GELU)
        ident = keep.tile([P, P], F32, name="ident")
        make_identity(nc, ident[:])

        x4 = xT.rearrange("(p j) t -> p j t", j=4)
        raw = []
        for j in range(4):
            raw.append(keep.tile([P, T], F32, name="raw%d" % j))
            nc.sync.dma_start(raw[j][:], x4[:, j, :])
            if j == 0:
                nc.sync.dma_start(offs_t[:], offs)
        w4 = w1.rearrange("(p j) c -> p j c", j=4)
        wraw = []
        for hh in range(4):
            wraw.append(keep.tile([P, 4, P], F32, name="wraw%d" % hh, align_bytes=64))
            nc.sync.dma_start(wraw[hh][:], w4[:, :, P * hh : P * hh + P])
        nc.sync.dma_start(par_t[:], par)
        share_t = []
        for hh in range(2):
            share_t.append(keep.tile([P, 512], F32, name="share%d" % hh, align_bytes=64))
            nc.sync.dma_start(share_t[hh][:], share[:, 512 * hh : 512 * hh + 512])
        w2w = keep.tile([P, 2 * N], U8, name="w2w", align_bytes=64)
        nc.sync.dma_start(w2w[:], w2_words[0])
        for q in range(4):
            nc.sync.dma_start(w2s[32 * q : 32 * q + 4, :].bitcast(I32), w2_scales[0, 4 * q : 4 * q + 4, :].bitcast(I32))

        rows = keep.tile([P, 4, BY_SCALAR], BF16, name="rows", align_bytes=64)
        xg_s = keep.tile([P, 4 * BY_SCALAR], BF16, name="xg_s", align_bytes=64)
        xg_v = keep.tile([P, 4 * BY_VECTOR], BF16, name="xg_v", align_bytes=64)

        def pick_scalar(j, a, b):
            nc.scalar.activation(out=rows[:, j, a:b], in_=raw[j][:].indirect(offs_t[:, (BY_VECTOR + a) // 16 : (BY_VECTOR + b) // 16]), func=COPY)

        def lay(u, a, b):
            nc.gpsimd.tensor_copy(out=xg_s[:].rearrange("p (s j) -> p s j", j=4)[:, a:b, 2 * u : 2 * u + 2],
                                  in_=rows[:, 2 * u : 2 * u + 2, a:b].rearrange("p e s -> p s e"))

        for j in range(4):
            nc.vector.tensor_copy(out=xg_v[:].rearrange("p (s j) -> p s j", j=4)[:, :, j], in_=raw[j][:].indirect(offs_t[:, 0 : BY_VECTOR // 16]))
            if j < 3:
                pick_scalar(j, 0, BY_SCALAR)
            if j == 1:
                lay(0, 0, BY_SCALAR)
        for a, b in spans([P, BY_SCALAR - P]):
            pick_scalar(3, a, b)
            lay(1, a, b)

        wg = keep.tile([P, 4 * H], BF16, name="wg", align_bytes=64)

        def deal(hh, a, b):
            dst = wg[:].rearrange("p (t m i e) -> p m i t e", t=4, i=2, e=2)[:, 32 * hh : 32 * hh + 32, :, a:b, :]
            nc.scalar.copy(out=dst, in_=wraw[hh][:].rearrange("p (i e) (m t) -> p m i t e", e=2, t=4)[:, :, :, a:b, :])

        for hh in range(3):
            deal(hh, 0, 4)
        deal(3, 0, 2)
        deal(3, 2, 4)

        xs = keep.tile([P, S], U8, name="xs", align_bytes=64)
        xq_v = keep.tile([P, BY_VECTOR], U32, name="xq_v", align_bytes=64)
        xq_s = keep.tile([P, BY_SCALAR], U32, name="xq_s", tag="wraw3", align_bytes=64)
        ws = keep.tile([P, H], U8, name="ws", align_bytes=64)
        wq = keep.tile([P, H], U32, name="wq", align_bytes=64)

        def xq(a, b):
            return (xq_v[:, a:b] if a < BY_VECTOR else xq_s[:, a - BY_VECTOR : b - BY_VECTOR]).bitcast(FP8X4)

        def quant_x(a, b):
            part, first = (xg_v, 0) if a < BY_VECTOR else (xg_s, BY_VECTOR)
            nc.vector.quantize_mx(out=xq(a, b), scales=xs[:, a:b], in_=part[:, 4 * (a - first) : 4 * (b - first)])

        def quant_w(a, b):
            nc.vector.quantize_mx(out=wq[:, P * a : P * b].bitcast(FP8X4), scales=ws[:, P * a : P * b], in_=wg[:, 512 * a : 512 * b])

        quant_x(0, 512)
        quant_x(512, 640)
        quant_w(0, 1)
        quant_w(1, 2)
        quant_x(BY_VECTOR, S)
        quant_w(2, 4)

        h = [keep.tile([P, S], F32, name="h%d" % t, align_bytes=64) for t in range(4)]
        hd = keep.tile([P, 4, 256], F32, name="hd")
        for t in range(4):
            lhs = wq[:, P * t : P * t + P].bitcast(FP8X4)
            if t == 0:
                for (a, b), i in zip(((0, P), (P, 384), (384, 640), (768, S), (640, 768)), (3, 4, 5, 1, 2)):
                    acc = bank(i)[:, 0 : b - a]
                    nc.tensor.matmul_mx(out=acc, lhsT=lhs, lhsT_scale=ws[:, 0:P], rhs=xq(a, b), rhs_scale=xs[:, a:b], start=True, stop=True)
                    nc.scalar.activation(out=h[0][:, a:b], in_=acc, func=GELU)
            else:
                accs = [bank(i) for i in ((5, 4), (6, 7), (3, 5))[t - 1]]
                for a, b in spans([512, P, P, 256]):
                    nc.tensor.matmul_mx(out=accs[a // 512][:, a % 512 : a % 512 + b - a], lhsT=lhs, lhsT_scale=ws[:, P * t : P * t + P],
                                        rhs=xq(a, b), rhs_scale=xs[:, a:b], start=True, stop=True)
                    if b % 512 == 0:
                        nc.scalar.activation(out=h[t][:, b - 512 : b], in_=accs[a // 512][:], func=GELU)
            nc.sync.dma_start(hd[:, t, :], h[t][:, 768:S])

        def follow(dst, t, a, b):
            nc.vector.tensor_tensor(out=dst, in0=h[t][:].indirect(par_t[:, a // 16 : b // 16]), in1=share_t[a // 512][:, a % 512 : a % 512 + b - a], op=MULT)

        def turn(bk, e, src, first=False, last=False):
            for c in range(2):
                nc.tensor.matmul(out=bk[:, 256 * c + P * e : 256 * c + P * e + P], lhsT=src[:, P * c : P * c + P], rhs=ident[:], is_transpose=True,
                                 start=first and c == 0, stop=last and c == 1)

        def round_sums(bk, name):
            zt = keep.tile([P, 512], BF16, name=name, align_bytes=64)
            nc.scalar.copy(out=zt[:].rearrange("s (c p e) -> s c p e", c=2, e=2), in_=bk[:].rearrange("s (c e p) -> s c p e", c=2, e=2))
            return zt

        def turn_back(back, u, zt):
            for c in range(2):
                nc.tensor.transpose(back[:, 256 * c + P * u : 256 * c + P * u + P], zt[:].bitcast(F32)[:, P * c : P * c + P], ident[:])

        def weave(back, blocks, name):
            zg = keep.tile([P, 512 * blocks], BF16, name=name, align_bytes=64)
            nc.scalar.copy(out=zg[:].bitcast(F32).rearrange("p (c s u) -> p c s u", c=blocks, u=2), in_=back.rearrange("p (c u s) -> p c s u", c=blocks, u=2))
            return zg

        def add(zg, gg, hh):
            nc.vector.tensor_tensor(out=zg.rearrange("p (c i t) -> p c t i", i=4, t=4), in0=gg.rearrange("p t (c i) -> p c t i", i=4),
                                    in1=hh.rearrange("p t (c i) -> p c t i", i=4), op=ADD)

        def quant_z(parts, name, slot=None):
            n = sum(part.shape[1] for part in parts) // 4
            zq = keep.tile([P, n], U32, name="zq" + name, tag=slot or "zq" + name, align_bytes=64)
            zs = keep.tile([P, n], U8, name="zs" + name, align_bytes=64)
            for part, (a, b) in zip(parts, spans([part.shape[1] // 4 for part in parts])):
                nc.vector.quantize_mx(out=zq[:, a:b].bitcast(FP8X4), scales=zs[:, a:b], in_=part)
            return zq, zs

        def second(acc, mb, zq, zs):
            nc.tensor.matmul_mx(out=acc, lhsT=w2w[:, 256 * mb : 256 * mb + 256].bitcast(FP4X4), lhsT_scale=w2s[:, P * mb : P * mb + P],
                                rhs=zq[:].bitcast(FP8X4), rhs_scale=zs[:], start=True, stop=True)

        def product_two_banks(z, n, banks):
            accs = [bank(i)[:, 0:n] for i in banks]
            for mb in range(2):
                second(accs[mb], mb, *z)
            return accs

        sums = [[bank(1), bank(2), bank(0)], [bank(4), bank(6), bank(7)]]
        g = keep.tile([P, 4, 768], F32, name="g")

        def turn_all(src, t, **flag):
            for q in range(3):
                turn(sums[t // 2][q], t % 2, src[:, 256 * q : 256 * q + 256], **flag)

        turn_all(h[0], 0, first=True)
        turn_all(h[1], 1)
        follow(g[:, 0, 0:512], 0, 0, 512)
        follow(g[:, 0, 512:768], 0, 512, 768)
        turn_all(g[:, 0, :], 0)
        turn_all(h[2], 2, first=True)
        turn_all(h[3], 3)
        follow(g[:, 1, 0:512], 1, 0, 512)
        follow(g[:, 1, 512:768], 1, 512, 768)
        turn_all(g[:, 1, :], 1, last=True)
        zt = [round_sums(sums[0][q], "zt0%d" % q) for q in range(3)]
        plain = keep.tile([P, 256], F32, name="plain")
        nc.scalar.activation(out=plain[:], in_=h[0][:].indirect(par_t[:, 48:64]), func=COPY)
        backs = [bank(3), bank(5)]
        follow(g[:, 2, 0:512], 2, 0, 512)
        for q in range(2):
            turn(sums[1][q], 0, g[:, 2, 256 * q : 256 * q + 256])
        for q in range(3):
            follow(g[:, 3, 256 * q : 256 * q + 256], 3, 256 * q, 256 * q + 256)
            turn(sums[1][q], 1, g[:, 3, 256 * q : 256 * q + 256], last=q < 2)
            if q < 2:
                turn_back(backs[q], 0, zt[q])
        gd = keep.tile([P, 5, 256], F32, name="gd", tag="share0", align_bytes=64)
        follow(gd[:, 4, :], 2, 512, 768)
        turn(sums[1][2], 0, gd[:, 4, :], last=True)
        turn_back(backs[0], 1, round_sums(sums[1][0], "zt10"))
        backs.append(bank(4))
        turn_back(backs[2], 0, zt[2])
        for q in (1, 2):
            turn_back(backs[q], 1, round_sums(sums[1][q], "zt1%d" % q))
        zg0 = [weave(backs[0][:, 256 * c : 256 * c + 256], 1, "zg0%d" % c) for c in range(2)]
        zg1 = weave(backs[1][:], 2, "zg1")
        zg2 = [weave(backs[2][:, 256 * c : 256 * c + 256], 1, "zg2%d" % c) for c in range(2)]
        nc.vector.tensor_tensor(out=gd[:, 0, :], in0=plain[:], in1=share_t[1][:, 256:512], op=MULT)
        for t in range(1, 4):
            follow(gd[:, t, :], t, 768, S)
        out3 = out.rearrange("(mb p) s -> p mb s", mb=2)

        def finish_by_halves(z, a, banks):
            for mb, acc in enumerate(product_two_banks(z, 256, banks)):
                res = keep.tile([P, 256], F32, name="res%d_%d" % (a, mb))
                nc.scalar.copy(out=res[:], in_=acc)
                nc.sync.dma_start(out[P * mb : P * mb + P, a : a + 256], res[:])

        def finish(z, a, n, copy, i):
            acc = bank(i)
            for mb in range(2):
                second(acc[:, n * mb : n * mb + n], mb, *z)
            res = keep.tile([P, 2, n], F32, name="res%d" % a)
            copy(out=res[:], in_=acc[:, 0 : 2 * n].rearrange("p (mb s) -> p mb s", mb=2))
            nc.sync.dma_start(out3[:, :, a : a + n], res[:])

        nc.tensor.matmul_mx(out=bank(3)[:], lhsT=wq[:, 0:P].bitcast(FP8X4), lhsT_scale=ws[:, 0:P], rhs=xq(0, 512), rhs_scale=xs[:, 0:512], start=True, stop=True)
        finish_by_halves(quant_z([part[:] for part in zg0], "0"), 0, (1, 2))
        zg_d = [keep.tile([P, 512], BF16, name="zg_d%d" % q, tag=("zg00", "zg1")[q], align_bytes=64) for q in range(2)]
        add(zg_d[0][:], gd[:, 0:4, 0:P], hd[:, :, 0:P])
        finish_by_halves(quant_z([zg1[:]], "1"), 256, (7, 3))
        z_d0 = quant_z([zg_d[0][:]], "d0")
        add(zg_d[1][:], gd[:, 0:4, P : 2 * P], hd[:, :, P : 2 * P])
        z_c0 = quant_z([zg2[0][:]], "c0")
        z_d1 = quant_z([zg_d[1][:]], "d1")
        z_c1 = quant_z([zg2[1][:]], "c1")
        finish(z_d0, 768, P, nc.scalar.copy, 0)
        finish(z_c0, 512, P, nc.scalar.copy, 6)
        finish(z_d1, 896, P, nc.vector.tensor_copy, 5)
        accs = product_two_banks(z_c1, P, (4, 1))
        res = keep.tile([P, 2, P], F32, name="res_last")
        nc.scalar.copy(out=res[:, 0, :], in_=accs[0])
        nc.vector.tensor_copy(out=res[:, 1, :], in_=accs[1])
        nc.sync.dma_start(out3[:, :, 640:768], res[:])
